import numpy as np
import ml_dtypes


def mxq(x, axis, fmt="e4m3"):
    dtype, down = {"e4m3": (ml_dtypes.float8_e4m3fn, 7), "e5m2": (ml_dtypes.float8_e5m2, 14)}[fmt]
    v = np.moveaxis(np.asarray(x, np.float32).astype(ml_dtypes.bfloat16).astype(np.float64), axis, -1)
    blocks = v.reshape(v.shape[:-1] + (-1, 32))
    amax = np.abs(blocks).max(-1, keepdims=True)
    byte = np.maximum(np.where(amax > 0, np.frexp(amax)[1] - 1 + 127, 0) - down, 1)
    scale = np.exp2(byte - 127.0)
    codes = (blocks / scale).astype(np.float32).astype(dtype).astype(np.float64)
    return np.moveaxis((codes * scale).reshape(v.shape), -1, axis)


WIDE = False


def mx_kscale(k):
    if not WIDE:
        return np.ones(k)
    levels = np.array([10, -10, 5, -5, 0])
    if k % 512:
        return np.exp2(np.random.permutation(np.resize(levels, k // 32))).repeat(32)
    a = np.empty((k // 512, 16))
    for p in range(k // 512):
        a[p, :8] = np.random.permutation(np.resize(levels, 8))
        for g in range(8):
            far = levels[np.abs(levels - a[p, g]) >= 10]
            a[p, g + 8] = far[np.random.randint(len(far))]
    return np.exp2(a.ravel()).repeat(32)


BF16 = ml_dtypes.bfloat16


def bf(x):
    return np.asarray(x, np.float32).astype(BF16)


def f64(x):
    return np.asarray(x).astype(np.float64)


E2M1 = np.array([0.0, 0.5, 1.0, 1.5, 2.0, 3.0, 4.0, 6.0, -0.0, -0.5, -1.0, -1.5, -2.0, -3.0, -4.0, -6.0])


def pack_weight(w, fmt):
    k, n = w.shape
    w = f64(bf(w)).reshape(k // 32, 32, n)
    amax = np.abs(w).max(1)
    if fmt == "e4m3":
        byte = np.frexp(amax)[1] - 1 + 127 - 7
    else:
        mant, ex = np.frexp(amax / 6.0)
        byte = np.where(mant > 0.5, ex, ex - 1) + 127
    byte = np.clip(np.where(amax > 0, byte, 1), 1, 254)
    scaled = (w * np.exp2(127.0 - byte)[:, None, :]).reshape(k, n).astype(np.float32)
    by_word = np.ascontiguousarray(scaled.reshape(k // 512, 128, 4, n).transpose(0, 1, 3, 2))
    if fmt == "e4m3":
        words = by_word.astype(ml_dtypes.float8_e4m3fn).view(np.uint8)
    else:
        c = by_word.astype(ml_dtypes.float4_e2m1fn).view(np.uint8) & 0xF
        words = c[..., 0::2] | (c[..., 1::2] << 4)
    return np.ascontiguousarray(words), np.ascontiguousarray(byte.astype(np.uint8).reshape(k // 512, 16, n))


def unpack_weight(words, scales, fmt):
    g, p, n, _ = words.shape
    if fmt == "e4m3":
        vals = np.ascontiguousarray(words).view(ml_dtypes.float8_e4m3fn).astype(np.float64)
    else:
        nib = np.empty((g, p, n, 4), np.uint8)
        nib[..., 0::2] = words & 0xF
        nib[..., 1::2] = words >> 4
        vals = E2M1[nib]
    vals = vals * np.repeat(np.exp2(scales.astype(np.float64) - 127.0), 8, axis=1)[..., None]
    return vals.transpose(0, 1, 3, 2).reshape(g * 512, n)
def pack4(w):
    words, scales = pack_weight(w, "e2m1")
    return words.reshape(words.shape[0], 128, -1), scales


def unpack4(words, scales):
    return unpack_weight(words.reshape(words.shape[0], 128, -1, 2), scales, "e2m1")


E4M3FN = np.array([(-1.0 if i & 128 else 1.0) * ((1.0 + (i & 7) / 8.0) * 2.0 ** (((i >> 3) & 15) - 7) if i & 120 else (i & 7) * 2.0 ** -9) for i in range(256)])


def e4m3fn_bytes(y):
    return np.clip(np.asarray(y, np.float64), -448.0, 448.0).astype(np.float32).astype(ml_dtypes.float8_e4m3fn).view(np.uint8)


def e4m3fn_values(b):
    return E4M3FN[b]


P, E, F, G, A = 2048, 1024, 1024, 8, 16
K = G * A
C = 2 * K
N = K - 1


def erf(a):
    c = np.clip(a, -6.0, 6.0)
    q = 2.0 * c * c
    term = c.copy()
    total = c.copy()
    for n in range(1, 150):
        term *= q
        term /= 2.0 * n + 1.0
        total += term
    return np.where(np.abs(a) > 6.0, np.sign(a), 2.0 / np.sqrt(np.pi) * np.exp(-c * c) * total)


def gelu_erf(v):
    return 0.5 * v * (1.0 + erf(v / np.sqrt(2.0)))


def softplus(v):
    return np.maximum(v, 0.0) + np.log(1.0 + np.exp(-np.abs(v)))


def log_binomial_stirling():
    eps = 1e-6
    n = float(N)
    k = np.arange(K, dtype=np.float64)
    lower = k + eps
    upper = n - k + eps
    return n * np.log(n) - lower * np.log(lower) - upper * np.log(upper)


def draw0():
    s, t = mx_kscale(E), mx_kscale(F)
    x = bf(np.random.standard_normal((P, E)) * s)
    w1_words, w1_scales = pack4(np.random.standard_normal((E, F)) / np.sqrt(E) / s[:, None])
    b1 = bf(np.random.standard_normal(F) * 0.3)
    g = bf(np.random.standard_normal(F) * t)
    w_head_words, w_head_scales = pack4(np.random.standard_normal((F, C)) * 2.0 / np.sqrt(F) / t[:, None])
    w_q = bf(np.random.standard_normal(F) / np.sqrt(F) / t)
    return {
        "x": x,
        "w1_words": w1_words,
        "w1_scales": w1_scales,
        "b1": b1,
        "g": g,
        "w_head_words": w_head_words,
        "w_head_scales": w_head_scales,
        "w_q": w_q,
    }


def core(x, w1_words, w1_scales, b1, g, w_head_words, w_head_scales, w_q):
    rows = x.shape[0]

    h = gelu_erf((mxq(f64(x), 1, "e4m3") @ unpack4(w1_words, w1_scales)) + f64(b1)) * f64(g)

    y = softplus(mxq(h, 1, "e4m3") @ unpack4(w_head_words, w_head_scales))
    c = y[:, :K].reshape(rows, G, A)
    a = y[:, K:C].reshape(rows, G, A)

    dx = a[:, :, None, :] - c[:, :, :, None]
    pull = np.mean(dx / (1.0 + 2.0 * dx ** 2), axis=-1)
    c2 = (c + 2.0 * pull).reshape(rows, K)

    u = np.sum(h * f64(w_q)[None, :], axis=-1)

    lc = log_binomial_stirling()

    k = np.arange(K, dtype=np.float64)
    logits = (lc[None, :] + k[None, :] * u[:, None]) / 20.0
    e = np.exp(logits - logits.max(axis=-1, keepdims=True))
    p = e / e.sum(axis=-1, keepdims=True)

    return K * p * c2


def setup_inputs():
    drawn = draw0()
    full = np.asarray(drawn['x']).astype(np.float64)
    scale = (np.abs(full).reshape(2048, 8, 128).max(axis=(2,)) / 448.0).astype(np.float32)
    given = {}
    for key, value in drawn.items():
        if key == 'x':
            given['x_bytes'] = e4m3fn_bytes(full / np.repeat(scale.astype(np.float64), 128, axis=1))
            given['x_scale'] = scale
        else:
            given[key] = value
    return given


def reference(x_bytes, x_scale, w1_words, w1_scales, b1, g, w_head_words, w_head_scales, w_q):
    return core(e4m3fn_values(x_bytes) * np.repeat(x_scale.astype(np.float64), 128, axis=1), w1_words, w1_scales, b1, g, w_head_words, w_head_scales, w_q)

@@ -1,0 +1,615 @@
+import math
+from contextlib import ExitStack
+
+import concourse.mybir as mybir
+from concourse.masks import make_identity
+
+F32 = mybir.dt.float32
+BF16 = mybir.dt.bfloat16
+I32 = mybir.dt.int32
+U32 = mybir.dt.uint32
+U8 = mybir.dt.uint8
+E4M3 = mybir.dt.float8_e4m3fn
+FP8X4 = mybir.dt.float8_e4m3fn_x4
+FP4X4 = mybir.dt.float4_e2m1fn_x4
+ALU = mybir.AluOpType
+ACT = mybir.ActivationFunctionType
+AX = mybir.AxisListType
+
+P = 128
+TOK, E, F, G, A = 2048, 1024, 1024, 8, 16
+K = G * A
+CH = 512
+NCH = TOK // CH
+NT = CH // P
+TILES = NCH * NT
+PAIRS = A // 2
+KB4 = 1024
+
+RHO_TWICE = (3, 5, 7, 9, 11, 13)
+S_WIDEN = 0
+S_WIDEN_HEAD = 3
+
+FLOPS = 2 * TOK * E * F + 2 * TOK * F * 2 * K + 2 * TOK * F + 12 * TOK * K * A
+
+
+def tile_attractordepthbinhead_d1p_kernel(
+    tc, x_bytes, x_scale, w1_words, w1_scales, b1, g, w_head_words, w_head_scales, w_q, out
+):
+    nc = tc.nc
+    with ExitStack() as ctx:
+        keep = ctx.enter_context(tc.tile_pool(name="keep", bufs=1))
+        work = ctx.enter_context(tc.tile_pool(name="work", bufs=2))
+        psum = ctx.enter_context(tc.psum_pool(name="psum", bufs=4))
+        side = ctx.enter_context(tc.psum_pool(name="side", bufs=4))
+        ctx.enter_context(tc.manual_schedule())
+
+        def t4(name):
+            return work.tile([P, KB4], F32, name=name, tag="t4", bufs=12, align_bytes=64)
+
+        xsc = keep.tile([P, NCH, NT, 8], F32, name="xsc")
+        nc.scalar.dma_start(out=xsc[:], in_=x_scale.rearrange("(c p a) j -> p c a j", p=P, a=NT))
+        vecs = []
+        for i, v in enumerate((b1, g, w_q)):
+            vec = keep.tile([P, 2, 4], BF16, name="vec%d" % i)
+            nc.scalar.dma_start(out=vec[:], in_=v.rearrange("(h p t) -> p h t", h=2, t=4))
+            vecs.append(vec)
+
+        w1raw = keep.tile([P, 2, 2 * F], U8, name="w1raw")
+        w1sraw = keep.tile([P, 2, F], U8, name="w1sraw", align_bytes=64)
+        wh = keep.tile([P, 2, 4 * K], U8, name="wh", align_bytes=64)
+        whs = keep.tile([P, 2, 2 * K], U8, name="whs", align_bytes=64)
+        nc.vector.memset(w1sraw[:].rearrange("p h n -> p (h n)").bitcast(I32), 0)
+        nc.gpsimd.memset(whs[:].rearrange("p h n -> p (h n)").bitcast(I32), 0)
+
+        xbs = {}
+
+        def load_x(c, pieces=1):
+            xb = work.tile([P, NT, E], U8, name="xb", bufs=3)
+            xbs[c] = xb
+            src = x_bytes[c * CH : (c + 1) * CH, :].rearrange("(p a) k -> p a k", a=NT)
+            n = NT // pieces
+            for i in range(pieces):
+                nc.sync.dma_start(out=xb[:, i * n : (i + 1) * n, :], in_=src[:, i * n : (i + 1) * n, :])
+
+        def load_scales(dst, src):
+            for h in range(2):
+                for q in range(4):
+                    nc.sync.dma_start(
+                        out=dst[32 * q : 32 * q + 4, h, :].bitcast(I32), in_=src[h, 4 * q : 4 * q + 4, :].bitcast(I32)
+                    )
+
+        load_x(0, 2)
+        nc.sync.dma_start(out=w1raw[:], in_=w1_words.rearrange("h p n -> p h n"))
+        load_scales(w1sraw, w1_scales)
+        load_x(1)
+        nc.sync.dma_start(out=wh[:], in_=w_head_words.rearrange("h p n -> p h n"))
+        load_scales(whs, w_head_scales)
+        load_x(2)
+
+        ident = keep.tile([P, P], F32, name="ident")
+        make_identity(nc, ident[:])
+        w1p = keep.tile([P, 2, 2 * F], U8, name="w1p", align_bytes=64)
+        w1s = keep.tile([P, 2, F], U8, name="w1s", align_bytes=64)
+
+        def permute_words(hh):
+            for kg in range(2):
+                nc.vector.tensor_copy(
+                    out=w1p[:, kg, hh * F : (hh + 1) * F].rearrange("p (t m b) -> p t m b", t=4, b=2),
+                    in_=w1raw[:, kg, hh * F : (hh + 1) * F].rearrange("p (m t b) -> p t m b", t=4, b=2),
+                )
+
+        def permute_scales(hh, eng):
+            for kg in range(2):
+                eng.tensor_copy(
+                    out=w1s[:, kg, hh * 512 : (hh + 1) * 512].rearrange("p (t m) -> p t m", t=4),
+                    in_=w1sraw[:, kg, hh * 512 : (hh + 1) * 512].rearrange("p (m t) -> p t m", t=4),
+                )
+
+        vecf = keep.tile([P, 3, 8], F32, name="vecf")
+        gw = keep.tile([P, 8], F32, name="gw")
+
+        rot = keep.tile([P, 2 * A, G], F32, name="rot")
+        back = keep.tile([P, G, A], F32, name="back")
+        rotf = rot[:].rearrange("p i q -> p (i q)")
+        backf = back[:].rearrange("p q i -> p (q i)")
+        fbufs = [keep.tile([P, 9 * P], F32, name="fb%d" % i) for i in range(3)]
+        kk = keep.tile([P, K], F32, name="kk")
+
+        def gpsimd_constants():
+            for d in range(2):
+                nc.gpsimd.tensor_copy(
+                    out=rot[:, d * A : (d + 1) * A, :], in_=ident[:].rearrange("p (q i) -> p i q", i=A)
+                )
+            nc.gpsimd.tensor_copy(out=back[:], in_=ident[:].rearrange("p (i q) -> p q i", i=A))
+            for fb in fbufs:
+                nc.gpsimd.memset(fb[:], 0.0)
+
+        def turned(r):
+            return rotf[:, r * G : r * G + P]
+
+        xgs = {}
+        xss = {}
+
+        def widen(c, a, on_scalar):
+            xs = work.tile([P, E], BF16, name="xs", bufs=4)
+            xss[c, a] = xs
+            for j in range(8):
+                src = xbs[c][:, a, j * P : (j + 1) * P].bitcast(E4M3)
+                sc = xsc[:, c, a, j : j + 1]
+                dst = xs[:, j * P : (j + 1) * P]
+                if j >= 8 - on_scalar:
+                    nc.scalar.activation(out=dst, in_=src, func=ACT.Copy, scale=sc)
+                else:
+                    nc.vector.tensor_scalar(out=dst, in0=src, scalar1=sc, scalar2=None, op0=ALU.mult)
+
+        def turn_x(c, a):
+            if a == 0:
+                xgs[c] = [t4("xg0"), t4("xg1")]
+            xt = psum.tile([P, 4, P], F32, name="bank")
+            words = xss[c, a][:].bitcast(F32)
+            for kg in range(2):
+                for u in range(2):
+                    nc.tensor.transpose(xt[:, 2 * kg + u, :], words[:, 256 * kg + u : 256 * (kg + 1) : 2], ident[:])
+            for kg in range(2):
+                nc.scalar.copy(
+                    out=xgs[c][kg][:, 2 * a * P : 2 * (a + 1) * P].rearrange("p (r u) -> p r u", u=2),
+                    in_=xt[:, 2 * kg : 2 * kg + 2, :].rearrange("p u r -> p r u"),
+                )
+
+        xqs = {}
+        hqs = {}
+
+        def quantize(key, store, kg, src):
+            if kg == 0:
+                store[key] = (
+                    work.tile([P, 2, CH], U32, name="codes", bufs=4, align_bytes=64),
+                    work.tile([P, 2, CH], U8, name="scales", bufs=4, align_bytes=64),
+                )
+            codes, scales = store[key]
+            nc.vector.quantize_mx(out=codes[:, kg, :].bitcast(FP8X4), scales=scales[:, kg, :], in_=src)
+
+        def quantize_x(c, kg):
+            quantize(c, xqs, kg, xgs[c][kg][:].bitcast(BF16))
+
+        gels = {}
+        hbs = {}
+
+        def first(c, hh):
+            gel = work.tile([P, 4, CH], F32, name="gel", bufs=8)
+            gels[c, hh] = gel
+            codes, scales = xqs[c]
+            for t in range(4):
+                ps = psum.tile([P, CH], F32, name="bank")
+                for kg in range(2):
+                    b0 = hh * F + t * 2 * P
+                    s0 = hh * 512 + t * P
+                    nc.tensor.matmul_mx(
+                        out=ps[:],
+                        lhsT=w1p[:, kg, b0 : b0 + 2 * P].bitcast(FP4X4),
+                        lhsT_scale=w1s[:, kg, s0 : s0 + P],
+                        rhs=codes[:, kg, :].bitcast(FP8X4),
+                        rhs_scale=scales[:, kg, :],
+                        start=(kg == 0),
+                        stop=(kg == 1),
+                    )
+                nc.scalar.activation(
+                    out=gel[:, t, :], in_=ps[:], func=ACT.Gelu, bias=vecf[:, 0, 4 * hh + t : 4 * hh + t + 1]
+                )
+
+        def gain(c, hh):
+            hb = t4("hb")
+            hbs[c, hh] = hb
+            nc.vector.tensor_tensor(
+                out=hb[:].bitcast(BF16).rearrange("p (n t) -> p n t", t=4),
+                in0=gels[c, hh][:].rearrange("p t n -> p n t"),
+                in1=vecf[:, 1, 4 * hh : 4 * hh + 4].unsqueeze(1).to_broadcast([P, CH, 4]),
+                op=ALU.mult,
+            )
+
+        def quantize_h(c, hh):
+            quantize(c, hqs, hh, hbs[c, hh][:].bitcast(BF16))
+
+        yps = {}
+
+        def second(c):
+            codes, scales = hqs[c]
+            for s in range(2):
+                y = side.tile([P, CH], F32, name="side")
+                yps[c, s] = y
+                for hh in range(2):
+                    nc.tensor.matmul_mx(
+                        out=y[:],
+                        lhsT=wh[:, hh, s * 2 * P : (s + 1) * 2 * P].bitcast(FP4X4),
+                        lhsT_scale=whs[:, hh, s * P : (s + 1) * P],
+                        rhs=codes[:, hh, :].bitcast(FP8X4),
+                        rhs_scale=scales[:, hh, :],
+                        start=(hh == 0),
+                        stop=(hh == 1),
+                    )
+
+        aT = keep.tile([P, TOK], F32, name="aT")
+        nc2T = keep.tile([P, TOK], F32, name="nc2T")
+        sp = {}
+        dup = {}
+
+        def softplus_abs(c):
+            sp[c] = t4("e")
+            for s in range(2):
+                nc.scalar.activation(out=sp[c][:, s * CH : (s + 1) * CH], in_=yps[c, s][:], func=ACT.Abs)
+
+        def softplus_exp(c):
+            nc.scalar.activation(out=sp[c][:], in_=sp[c][:], func=ACT.Exp, scale=-1.0)
+
+        def softplus_ln(c):
+            nc.scalar.activation(out=sp[c][:], in_=sp[c][:], func=ACT.Ln, bias=1.0)
+
+        def softplus_sum(c):
+            e = sp[c]
+            cs = slice(c * CH, (c + 1) * CH)
+            nc.vector.scalar_tensor_tensor(
+                out=aT[:, cs], in0=yps[c, 1][:], scalar=0.0, in1=e[:, CH:KB4], op0=ALU.max, op1=ALU.add
+            )
+            nc.vector.scalar_tensor_tensor(
+                out=e[:, 0:CH], in0=yps[c, 0][:], scalar=0.0, in1=e[:, 0:CH], op0=ALU.max, op1=ALU.add
+            )
+
+        def softplus_end(c):
+            cs = slice(c * CH, (c + 1) * CH)
+            nc.vector.tensor_scalar(out=nc2T[:, cs], in0=sp[c][:, 0:CH], scalar1=-2.0, scalar2=None, op0=ALU.mult)
+
+        tps = {}
+
+        def pair_turn(c):
+            tp = side.tile([P, NT, P], F32, name="side")
+            tps[c] = tp
+            for a in range(NT):
+                i = c * NT + a
+                nc.tensor.transpose(tp[:, a, :], aT[:, i * P : (i + 1) * P], ident[:])
+
+        def pair_consts(c, eng):
+            tp = tps[c]
+            al = work.tile([P, NT, G, A], F32, name="al")
+            nc.vector.tensor_copy(out=al[:].rearrange("p a q i -> p (a q i)"), in_=tp[:].rearrange("p a k -> p (a k)"))
+            d2 = work.tile([P, PAIRS, NT * G], F32, name="d2")
+            ai = al[:].rearrange("p a q i -> p i (a q)")
+            eng.tensor_tensor(out=d2[:], in0=ai[:, 0:PAIRS], in1=ai[:, PAIRS:A], op=ALU.subtract)
+            d2f = d2[:].rearrange("p j x -> p (j x)")
+            eng.tensor_tensor(out=d2f, in0=d2f, in1=d2f, op=ALU.mult)
+            bg = work.tile([P, 2, 2 * PAIRS, NT, G], F32, name="bg", bufs=3)
+            src = d2f.unsqueeze(1).to_broadcast([P, 2, PAIRS * NT * G])
+            for v, (s1, s2) in enumerate(((-1.0, 2.0), (8.0, 0.0))):
+                eng.tensor_scalar(
+                    out=bg[:, v].rearrange("p (h j) a q -> p h (j a q)", h=2), in0=src, scalar1=s1, scalar2=s2,
+                    op0=ALU.mult, op1=ALU.add,
+                )
+            dup[c] = bg
+
+        lc = keep.tile([P, K], F32, name="lc")
+        lo = keep.tile([P, K], F32, name="lo")
+        up = keep.tile([P, K], F32, name="up")
+        l1 = keep.tile([P, K], F32, name="l1")
+        l2 = keep.tile([P, K], F32, name="l2")
+
+        def binomial_start():
+            n = float(K - 1)
+            nc.vector.tensor_scalar(out=lo[:], in0=kk[:], scalar1=1e-6, scalar2=None, op0=ALU.add)
+            nc.vector.tensor_scalar(out=up[:], in0=kk[:], scalar1=-1.0, scalar2=n, op0=ALU.mult, op1=ALU.add)
+            nc.vector.tensor_scalar(out=up[:], in0=up[:], scalar1=1e-6, scalar2=None, op0=ALU.add)
+
+        def binomial_ln():
+            nc.scalar.activation(out=l1[:], in_=lo[:], func=ACT.Ln)
+            nc.scalar.activation(out=l2[:], in_=up[:], func=ACT.Ln)
+
+        def binomial_end():
+            n = float(K - 1)
+            nc.vector.tensor_mul(out=l1[:], in0=l1[:], in1=lo[:])
+            nc.vector.tensor_mul(out=l2[:], in0=l2[:], in1=up[:])
+            nc.vector.tensor_add(out=l1[:], in0=l1[:], in1=l2[:])
+            nc.vector.tensor_scalar(
+                out=lc[:], in0=l1[:], scalar1=-1.0, scalar2=n * math.log(n), op0=ALU.mult, op1=ALU.add
+            )
+
+        us = keep.tile([P, TILES], F32, name="us")
+        ssum = keep.tile([P, TILES], F32, name="ssum")
+        rs = keep.tile([P, TILES], F32, name="rs")
+        mx = keep.tile([P, TILES], F32, name="mx")
+        lgs = [keep.tile([P, NT, K], F32, name="lg%d" % c) for c in range(NCH)]
+        uts = {}
+
+        def u_tile(i, pool=side):
+            c, a = divmod(i, NT)
+            if a % 2 == 0:
+                uts[i // 2] = pool.tile([P, 2], F32, name="bank" if pool is psum else "side")
+            for m in range(8):
+                nc.tensor.matmul(
+                    out=uts[i // 2][:, a % 2 : a % 2 + 1],
+                    lhsT=gels[c, m // 4][:, m % 4, a * P : (a + 1) * P],
+                    rhs=gw[:, m : m + 1],
+                    start=(m == 0),
+                    stop=(m == 7),
+                )
+
+        def u_out(h):
+            nc.vector.tensor_copy(out=us[:, 2 * h : 2 * h + 2], in_=uts[h][:])
+
+        def logits(c):
+            for a in range(NT):
+                i = c * NT + a
+                nc.vector.scalar_tensor_tensor(
+                    out=lgs[c][:, a, :], in0=kk[:], scalar=us[:, i : i + 1], in1=lc[:], op0=ALU.mult, op1=ALU.add
+                )
+            cols = slice(c * NT, (c + 1) * NT)
+            nc.vector.tensor_reduce(out=mx[:, cols], in_=lgs[c][:], axis=AX.X, op=ALU.max)
+            nc.vector.tensor_scalar(out=mx[:, cols], in0=mx[:, cols], scalar1=-1.0 / 20.0, scalar2=None, op0=ALU.mult)
+
+        def softmax_exp(c):
+            for a in range(NT):
+                i = c * NT + a
+                nc.scalar.activation(
+                    out=lgs[c][:, a, :], in_=lgs[c][:, a, :], func=ACT.Exp, bias=mx[:, i : i + 1], scale=1.0 / 20.0,
+                    accum_out=ssum[:, i : i + 1],
+                )
+
+        def softmax_end():
+            nc.vector.reciprocal(out=rs[:], in_=ssum[:])
+            nc.vector.tensor_scalar(out=rs[:], in0=rs[:], scalar1=-64.0, scalar2=None, op0=ALU.mult)
+
+        xps = {}
+        qs = {}
+        ns = {}
+        n2s = {}
+        pulls = {}
+
+        def at_x(i):
+            ts = slice(i * P, (i + 1) * P)
+            xps[i] = []
+            for b in range(2):
+                xp = psum.tile([P, 4, P], F32, name="bank")
+                xps[i].append(xp)
+                for rr in range(4):
+                    terms = ((aT, 0), (aT, PAIRS), (nc2T, 4 * b + rr))
+                    for k, (src, turn) in enumerate(terms):
+                        nc.tensor.matmul(
+                            out=xp[:, rr, :], lhsT=src[:, ts], rhs=turned(turn), is_transpose=True,
+                            start=(k == 0), stop=(k == 2),
+                        )
+
+        def at_q(i):
+            qs[i] = t4("q")
+            for b in range(2):
+                nc.scalar.activation(
+                    out=qs[i][:, b * 512 : (b + 1) * 512], in_=xps[i][b][:].rearrange("p r k -> p (r k)"), func=ACT.Square
+                )
+
+        def row(i, v):
+            c, a = divmod(i, NT)
+            return dup[c][:, v, :, a, :].unsqueeze(1).to_broadcast([P, PAIRS, A, G])
+
+        def rk(t):
+            return t[:].rearrange("p (r k) -> p r k", k=P)
+
+        def rsq(t):
+            return t[:].rearrange("p (r s q) -> p r s q", s=A, q=G)
+
+        def at_n(i):
+            ns[i] = t4("n")
+            nc.vector.tensor_add(out=rsq(ns[i]), in0=rsq(qs[i]), in1=row(i, 0))
+
+        def at_n2(i):
+            n2s[i] = t4("n2")
+            nc.scalar.activation(out=n2s[i][:], in_=ns[i][:], func=ACT.Square)
+
+        def at_xn(i):
+            for b in range(2):
+                half = slice(b * 512, (b + 1) * 512)
+                nc.vector.tensor_mul(
+                    out=qs[i][:, half], in0=xps[i][b][:].rearrange("p r k -> p (r k)"), in1=ns[i][:, half]
+                )
+
+        def at_d(i):
+            nc.gpsimd.tensor_tensor(out=rsq(n2s[i]), in0=rsq(n2s[i]), in1=row(i, 1), op=ALU.add)
+
+        def at_rho(i):
+            nc.scalar.activation(out=n2s[i][:], in_=n2s[i][:], func=ACT.Abs_reciprocal_sqrt)
+
+        def at_r(i):
+            if i in RHO_TWICE:
+                nc.vector.tensor_mul(out=qs[i][:], in0=qs[i][:], in1=n2s[i][:])
+            else:
+                nc.scalar.activation(out=n2s[i][:], in_=n2s[i][:], func=ACT.Square)
+
+        def at_f(i):
+            fb = fbufs[i % 3]
+            spread = fb[:, 0 : PAIRS * (P + G)].rearrange("p (r x) -> p r x", x=P + G)[:, :, 0:P]
+            nc.vector.tensor_mul(out=spread, in0=rk(qs[i]), in1=rk(n2s[i]))
+
+        def at_sum(i):
+            c, a = divmod(i, NT)
+            fb = fbufs[i % 3]
+            if a == 0:
+                pulls[c] = side.tile([P, NT, P], F32, name="side")
+            for r in range(PAIRS + 1):
+                nc.tensor.matmul(
+                    out=pulls[c][:, a, :], lhsT=fb[:, r * P : (r + 1) * P], rhs=ident[:], is_transpose=True,
+                    start=(r == 0), stop=(r == PAIRS),
+                )
+
+        pls = {}
+
+        def end_copy(c):
+            pls[c] = work.tile([P, CH], F32, name="pl")
+            nc.vector.tensor_scalar(
+                out=pls[c][:], in0=pulls[c][:].rearrange("p a k -> p (a k)"), scalar1=-0.5, scalar2=None, op0=ALU.mult
+            )
+
+        c2s = {}
+
+        def end_turn(c):
+            c2s[c] = side.tile([P, NT, P], F32, name="side")
+            for a in range(NT):
+                i = c * NT + a
+                nc.tensor.matmul(out=c2s[c][:, a, :], lhsT=pls[c][:, a * P : (a + 1) * P], rhs=backf, is_transpose=True, start=True, stop=False)
+                nc.tensor.matmul(out=c2s[c][:, a, :], lhsT=nc2T[:, i * P : (i + 1) * P], rhs=ident[:], is_transpose=True, start=False, stop=True)
+
+        def end_out(c):
+            o = work.tile([P, NT, K], F32, name="o")
+            for a in range(NT):
+                i = c * NT + a
+                nc.vector.scalar_tensor_tensor(
+                    out=o[:, a, :], in0=c2s[c][:, a, :], scalar=rs[:, i : i + 1], in1=lgs[c][:, a, :], op0=ALU.mult, op1=ALU.mult
+                )
+            nc.sync.dma_start(
+                out=out[c * CH : (c + 1) * CH, :].rearrange("(p a) k -> p a k", a=NT), in_=o[:]
+            )
+
+
+        nc.gpsimd.iota(kk[:], pattern=[[1, K]], base=0, channel_multiplier=0, allow_small_or_imprecise_dtypes=True)
+        permute_scales(0, nc.gpsimd)
+        permute_scales(1, nc.gpsimd)
+        gpsimd_constants()
+
+        def widen_pair(pr, on_scalar):
+            for w in (2 * pr, 2 * pr + 1):
+                widen(w // NT, w % NT, on_scalar)
+
+        def turn_pair(pr):
+            for w in (2 * pr, 2 * pr + 1):
+                turn_x(w // NT, w % NT)
+
+        for w in range(NT):
+            widen(0, w, 3)
+            turn_x(0, w)
+        for i in range(3):
+            nc.vector.tensor_copy(out=vecf[:, i, :], in_=vecs[i][:].rearrange("p h t -> p (h t)"))
+        permute_words(0)
+        for kg in range(2):
+            quantize_x(0, kg)
+        for j in range(2 * NCH):
+            first(j // 2, j % 2)
+            if j == 0:
+                permute_words(1)
+                widen_pair(2, 3)
+                turn_pair(2)
+            if j == 1:
+                load_x(3)
+            if j in (3, 5):
+                second((j - 3) // 2)
+            if j >= 1:
+                gain((j - 1) // 2, (j - 1) % 2)
+            if j >= 6:
+                u_out(j - 6)
+            if j == 7:
+                softplus_sum(0)
+            if j % 2 == 1 and j < 7:
+                quantize_x((j + 1) // 2, 0)
+            if j + 3 < 2 * NCH:
+                widen_pair(j + 3, 3)
+                turn_pair(j + 3)
+            if j % 2 == 1 and j < 7:
+                quantize_x((j + 1) // 2, 1)
+            if j >= 1:
+                quantize_h((j - 1) // 2, (j - 1) % 2)
+            if j == 1:
+                nc.vector.tensor_mul(out=gw[:], in0=vecf[:, 1, :], in1=vecf[:, 2, :])
+                binomial_start()
+            if j == 5:
+                softplus_abs(0)
+                softplus_abs(1)
+            if j == 6:
+                for b in (0, 1):
+                    softplus_exp(b)
+                for b in (0, 1):
+                    softplus_ln(b)
+                binomial_ln()
+            if j >= 5:
+                u_tile(2 * (j - 5), psum)
+                u_tile(2 * (j - 5) + 1, psum)
+        pair_turn(0)
+        softplus_end(0)
+        softplus_sum(1)
+        pair_consts(0, nc.gpsimd)
+        pair_turn(1)
+        softplus_end(1)
+        second(2)
+        gain(3, 1)
+        u_out(2)
+        binomial_end()
+        pair_consts(1, nc.gpsimd)
+
+        def attract_start(k):
+            at_x(k + 1)
+            at_q(k)
+            at_n(k)
+            at_n2(k)
+            at_xn(k)
+            at_d(k)
+
+        at_x(0)
+        attract_start(0)
+        quantize_h(3, 1)
+        second(3)
+        attract_start(1)
+        for c in (2, 3):
+            softplus_abs(c)
+        for c in (2, 3):
+            softplus_exp(c)
+        for c in (2, 3):
+            softplus_ln(c)
+        logits(0)
+        for c in (2, 3):
+            softplus_sum(c)
+        for c in (2, 3):
+            softplus_end(c)
+
+        def attract_step(k):
+            if k + 1 < TILES:
+                at_x(k + 1)
+            if k < TILES:
+                at_q(k)
+                at_n(k)
+            if 0 <= k - 3:
+                at_f(k - 3)
+            if 0 <= k - 2 < TILES:
+                at_rho(k - 2)
+            if k < TILES:
+                at_n2(k)
+                at_xn(k)
+                at_d(k)
+            if 0 <= k - 2 < TILES:
+                at_r(k - 2)
+
+        for k in range(2, TILES + 3):
+            d = k - 4
+            if k == 4:
+                pair_consts(2, nc.gpsimd)
+            if k == 9:
+                pair_consts(3, nc.gpsimd)
+            if d >= 0 and d % NT == NT - 1:
+                end_copy(d // NT)
+            if k in (4, 6, 8, 10, 12):
+                u_out((k + 2) // 2)
+            if k in (5, 9, 13):
+                logits((k - 1) // 4)
+            if k == 16:
+                for c in range(NCH):
+                    softmax_exp(c)
+            attract_step(k)
+            if k >= 3:
+                at_sum(k - 3)
+            if k == 17:
+                softmax_end()
+                end_out(0)
+                end_out(1)
+                end_out(2)
+            if d >= 0 and d % NT == NT - 1:
+                end_turn(d // NT)
+            if k == 2:
+                pair_turn(2)
+            if k == 8:
+                pair_turn(3)
+            if 2 <= k <= 11:
+                u_tile(6 + k - 2)
+        end_copy(3)
+        end_turn(3)
+        end_out(3)

@@ -26,9 +26,7 @@ TILES = NCH * NT
 PAIRS = A // 2
 KB4 = 1024
 
-RHO_TWICE = (3, 5, 7, 9, 11, 13)
-S_WIDEN = 0
-S_WIDEN_HEAD = 3
+T4_BUFS = 14
 
 FLOPS = 2 * TOK * E * F + 2 * TOK * F * 2 * K + 2 * TOK * F + 12 * TOK * K * A
 
@@ -40,12 +38,12 @@ def tile_attractordepthbinhead_d1p_kernel(
     with ExitStack() as ctx:
         keep = ctx.enter_context(tc.tile_pool(name="keep", bufs=1))
         work = ctx.enter_context(tc.tile_pool(name="work", bufs=2))
-        psum = ctx.enter_context(tc.psum_pool(name="psum", bufs=4))
-        side = ctx.enter_context(tc.psum_pool(name="side", bufs=4))
+        psum = ctx.enter_context(tc.psum_pool(name="psum", bufs=5))
+        side = ctx.enter_context(tc.psum_pool(name="side", bufs=3))
         ctx.enter_context(tc.manual_schedule())
 
         def t4(name):
-            return work.tile([P, KB4], F32, name=name, tag="t4", bufs=12, align_bytes=64)
+            return work.tile([P, KB4], F32, name=name, tag="t4", bufs=T4_BUFS, align_bytes=64)
 
         xsc = keep.tile([P, NCH, NT, 8], F32, name="xsc")
         nc.scalar.dma_start(out=xsc[:], in_=x_scale.rearrange("(c p a) j -> p c a j", p=P, a=NT))
@@ -92,19 +90,18 @@ def tile_attractordepthbinhead_d1p_kernel(
         w1p = keep.tile([P, 2, 2 * F], U8, name="w1p", align_bytes=64)
         w1s = keep.tile([P, 2, F], U8, name="w1s", align_bytes=64)
 
-        def permute_words(hh):
-            for kg in range(2):
-                nc.vector.tensor_copy(
-                    out=w1p[:, kg, hh * F : (hh + 1) * F].rearrange("p (t m b) -> p t m b", t=4, b=2),
-                    in_=w1raw[:, kg, hh * F : (hh + 1) * F].rearrange("p (m t b) -> p t m b", t=4, b=2),
-                )
-
-        def permute_scales(hh, eng):
-            for kg in range(2):
-                eng.tensor_copy(
-                    out=w1s[:, kg, hh * 512 : (hh + 1) * 512].rearrange("p (t m) -> p t m", t=4),
-                    in_=w1sraw[:, kg, hh * 512 : (hh + 1) * 512].rearrange("p (m t) -> p t m", t=4),
-                )
+        def permute(hh, t):
+            half = slice(hh * F, (hh + 1) * F)
+            nc.vector.tensor_copy(
+                out=w1p[:, :, half].rearrange("p k (t m b) -> p k t m b", t=4, b=2)[:, :, t],
+                in_=w1raw[:, :, half].rearrange("p k (m t b) -> p k t m b", t=4, b=2)[:, :, t],
+            )
+            half = slice(hh * 512, (hh + 1) * 512)
+            eng = nc.vector if hh == 0 else nc.gpsimd
+            eng.tensor_copy(
+                out=w1s[:, :, half].rearrange("p k (t m) -> p k t m", t=4)[:, :, t],
+                in_=w1sraw[:, :, half].rearrange("p k (m t) -> p k t m", t=4)[:, :, t],
+            )
 
         vecf = keep.tile([P, 3, 8], F32, name="vecf")
         gw = keep.tile([P, 8], F32, name="gw")
@@ -122,8 +119,6 @@ def tile_attractordepthbinhead_d1p_kernel(
                     out=rot[:, d * A : (d + 1) * A, :], in_=ident[:].rearrange("p (q i) -> p i q", i=A)
                 )
             nc.gpsimd.tensor_copy(out=back[:], in_=ident[:].rearrange("p (i q) -> p q i", i=A))
-            for fb in fbufs:
-                nc.gpsimd.memset(fb[:], 0.0)
 
         def turned(r):
             return rotf[:, r * G : r * G + P]
@@ -176,7 +171,7 @@ def tile_attractordepthbinhead_d1p_kernel(
         hbs = {}
 
         def first(c, hh):
-            gel = work.tile([P, 4, CH], F32, name="gel", bufs=8)
+            gel = work.tile([P, 4, CH], F32, name="gel", bufs=6)
             gels[c, hh] = gel
             codes, scales = xqs[c]
             for t in range(4):
@@ -228,15 +223,24 @@ def tile_attractordepthbinhead_d1p_kernel(
                         stop=(hh == 1),
                     )
 
-        aT = keep.tile([P, TOK], F32, name="aT")
+        aTs = {}
         nc2T = keep.tile([P, TOK], F32, name="nc2T")
         sp = {}
+        rl = {}
         dup = {}
 
-        def softplus_abs(c):
+        def leave_second(c):
             sp[c] = t4("e")
+            rl[c] = t4("rl")
             for s in range(2):
-                nc.scalar.activation(out=sp[c][:, s * CH : (s + 1) * CH], in_=yps[c, s][:], func=ACT.Abs)
+                half = slice(s * CH, (s + 1) * CH)
+                nc.scalar.activation(out=sp[c][:, half], in_=yps[c, s][:], func=ACT.Abs)
+                if c < NCH - 1:
+                    nc.scalar.activation(out=rl[c][:, half], in_=yps[c, s][:], func=ACT.Relu, scale=2.0 - s)
+                else:
+                    nc.vector.tensor_scalar(
+                        out=rl[c][:, half], in0=yps[c, s][:], scalar1=0.0, scalar2=2.0 - s, op0=ALU.max, op1=ALU.mult
+                    )
 
         def softplus_exp(c):
             nc.scalar.activation(out=sp[c][:], in_=sp[c][:], func=ACT.Exp, scale=-1.0)
@@ -244,42 +248,66 @@ def tile_attractordepthbinhead_d1p_kernel(
         def softplus_ln(c):
             nc.scalar.activation(out=sp[c][:], in_=sp[c][:], func=ACT.Ln, bias=1.0)
 
-        def softplus_sum(c):
-            e = sp[c]
-            cs = slice(c * CH, (c + 1) * CH)
-            nc.vector.scalar_tensor_tensor(
-                out=aT[:, cs], in0=yps[c, 1][:], scalar=0.0, in1=e[:, CH:KB4], op0=ALU.max, op1=ALU.add
-            )
-            nc.vector.scalar_tensor_tensor(
-                out=e[:, 0:CH], in0=yps[c, 0][:], scalar=0.0, in1=e[:, 0:CH], op0=ALU.max, op1=ALU.add
-            )
+        def softplus_a(c):
+            aTs[c] = work.tile([P, CH], F32, name="aT")
+            nc.vector.tensor_add(out=aTs[c][:], in0=rl[c][:, CH:KB4], in1=sp[c][:, CH:KB4])
 
-        def softplus_end(c):
-            cs = slice(c * CH, (c + 1) * CH)
-            nc.vector.tensor_scalar(out=nc2T[:, cs], in0=sp[c][:, 0:CH], scalar1=-2.0, scalar2=None, op0=ALU.mult)
+        def softplus_c(c):
+            nc.vector.scalar_tensor_tensor(
+                out=nc2T[:, c * CH : (c + 1) * CH], in0=sp[c][:, 0:CH], scalar=-2.0, in1=rl[c][:, 0:CH],
+                op0=ALU.mult, op1=ALU.subtract,
+            )
 
         tps = {}
+        m2s = {}
+        mps = {}
+        m2T = keep.tile([P, TOK], F32, name="m2T")
+
+        def mean_turn(c):
+            mp = side.tile([P, NT, P], F32, name="side")
+            m2f = m2s[c][:].rearrange("p x h j -> p (x h j)")
+            for a in range(NT):
+                nc.tensor.transpose(mp[:, a, :], m2f[:, a * P : (a + 1) * P], ident[:])
+            mps[c] = mp
+
+        def mean_copy(c):
+            nc.scalar.copy(out=m2T[:, c * CH : (c + 1) * CH], in_=mps[c][:].rearrange("p a k -> p (a k)"))
 
         def pair_turn(c):
             tp = side.tile([P, NT, P], F32, name="side")
             tps[c] = tp
             for a in range(NT):
-                i = c * NT + a
-                nc.tensor.transpose(tp[:, a, :], aT[:, i * P : (i + 1) * P], ident[:])
+                nc.tensor.transpose(tp[:, a, :], aTs[c][:, a * P : (a + 1) * P], ident[:])
 
-        def pair_consts(c, eng):
-            tp = tps[c]
-            al = work.tile([P, NT, G, A], F32, name="al")
-            nc.vector.tensor_copy(out=al[:].rearrange("p a q i -> p (a q i)"), in_=tp[:].rearrange("p a k -> p (a k)"))
+        als = {}
+
+        def pair_copy(c, on_scalar):
+            als[c] = work.tile([P, NT * G, A], F32, name="al")
+            out_, in_ = als[c][:].rearrange("p x i -> p (x i)"), tps[c][:].rearrange("p a k -> p (a k)")
+            if on_scalar:
+                nc.scalar.copy(out=out_, in_=in_)
+            else:
+                nc.vector.tensor_copy(out=out_, in_=in_)
+
+        def pair_means(c):
+            m2s[c] = work.tile([P, NT * G, 2, PAIRS], F32, name="m2", bufs=1)
+            both = [P, NT * G, 2, PAIRS]
+            nc.vector.tensor_add(
+                out=m2s[c][:],
+                in0=als[c][:, :, 0:PAIRS].unsqueeze(2).to_broadcast(both),
+                in1=als[c][:, :, PAIRS:A].unsqueeze(2).to_broadcast(both),
+            )
+
+        def pair_consts(c):
             d2 = work.tile([P, PAIRS, NT * G], F32, name="d2")
-            ai = al[:].rearrange("p a q i -> p i (a q)")
-            eng.tensor_tensor(out=d2[:], in0=ai[:, 0:PAIRS], in1=ai[:, PAIRS:A], op=ALU.subtract)
+            ai = als[c][:].rearrange("p x i -> p i x")
+            nc.vector.tensor_sub(out=d2[:], in0=ai[:, 0:PAIRS], in1=ai[:, PAIRS:A])
             d2f = d2[:].rearrange("p j x -> p (j x)")
-            eng.tensor_tensor(out=d2f, in0=d2f, in1=d2f, op=ALU.mult)
+            nc.vector.tensor_mul(out=d2f, in0=d2f, in1=d2f)
             bg = work.tile([P, 2, 2 * PAIRS, NT, G], F32, name="bg", bufs=3)
             src = d2f.unsqueeze(1).to_broadcast([P, 2, PAIRS * NT * G])
             for v, (s1, s2) in enumerate(((-1.0, 2.0), (8.0, 0.0))):
-                eng.tensor_scalar(
+                nc.vector.tensor_scalar(
                     out=bg[:, v].rearrange("p (h j) a q -> p h (j a q)", h=2), in0=src, scalar1=s1, scalar2=s2,
                     op0=ALU.mult, op1=ALU.add,
                 )
@@ -317,21 +345,26 @@ def tile_attractordepthbinhead_d1p_kernel(
         lgs = [keep.tile([P, NT, K], F32, name="lg%d" % c) for c in range(NCH)]
         uts = {}
 
-        def u_tile(i, pool=side):
-            c, a = divmod(i, NT)
-            if a % 2 == 0:
-                uts[i // 2] = pool.tile([P, 2], F32, name="bank" if pool is psum else "side")
-            for m in range(8):
-                nc.tensor.matmul(
-                    out=uts[i // 2][:, a % 2 : a % 2 + 1],
-                    lhsT=gels[c, m // 4][:, m % 4, a * P : (a + 1) * P],
-                    rhs=gw[:, m : m + 1],
-                    start=(m == 0),
-                    stop=(m == 7),
+        def weigh(c, hh):
+            gel = gels[c, hh]
+            for t in range(4):
+                m = 4 * hh + t
+                nc.vector.tensor_scalar(
+                    out=gel[:, t, :], in0=gel[:, t, :], scalar1=gw[:, m : m + 1], scalar2=None, op0=ALU.mult
                 )
 
-        def u_out(h):
-            nc.vector.tensor_copy(out=us[:, 2 * h : 2 * h + 2], in_=uts[h][:])
+        def u_turn(c, part):
+            if part == 0:
+                uts[c] = psum.tile([P, NT, P], F32, name="bank")
+            for a in (2 * part, 2 * part + 1):
+                for m in range(8):
+                    nc.tensor.matmul(
+                        out=uts[c][:, a, :], lhsT=gels[c, m // 4][:, m % 4, a * P : (a + 1) * P], rhs=ident[:],
+                        is_transpose=True, start=(m == 0), stop=(m == 7),
+                    )
+
+        def u_out(c):
+            nc.vector.tensor_reduce(out=us[:, c * NT : (c + 1) * NT], in_=uts[c][:], axis=AX.X, op=ALU.add)
 
         def logits(c):
             for a in range(NT):
@@ -368,11 +401,11 @@ def tile_attractordepthbinhead_d1p_kernel(
                 xp = psum.tile([P, 4, P], F32, name="bank")
                 xps[i].append(xp)
                 for rr in range(4):
-                    terms = ((aT, 0), (aT, PAIRS), (nc2T, 4 * b + rr))
+                    terms = ((m2T, 0), (nc2T, 4 * b + rr))
                     for k, (src, turn) in enumerate(terms):
                         nc.tensor.matmul(
                             out=xp[:, rr, :], lhsT=src[:, ts], rhs=turned(turn), is_transpose=True,
-                            start=(k == 0), stop=(k == 2),
+                            start=(k == 0), stop=(k == 1),
                         )
 
         def at_q(i):
@@ -394,7 +427,9 @@ def tile_attractordepthbinhead_d1p_kernel(
 
         def at_n(i):
             ns[i] = t4("n")
-            nc.vector.tensor_add(out=rsq(ns[i]), in0=rsq(qs[i]), in1=row(i, 0))
+            for b in range(2):
+                half = slice(b * PAIRS // 2, (b + 1) * PAIRS // 2)
+                nc.vector.tensor_add(out=rsq(ns[i])[:, half], in0=rsq(qs[i])[:, half], in1=row(i, 0)[:, half])
 
         def at_n2(i):
             n2s[i] = t4("n2")
@@ -408,66 +443,64 @@ def tile_attractordepthbinhead_d1p_kernel(
                 )
 
         def at_d(i):
-            nc.gpsimd.tensor_tensor(out=rsq(n2s[i]), in0=rsq(n2s[i]), in1=row(i, 1), op=ALU.add)
+            nc.vector.tensor_add(out=rsq(n2s[i]), in0=rsq(n2s[i]), in1=row(i, 1))
 
-        def at_rho(i):
-            nc.scalar.activation(out=n2s[i][:], in_=n2s[i][:], func=ACT.Abs_reciprocal_sqrt)
+        def at_rho(i, part=slice(0, KB4)):
+            nc.scalar.activation(out=n2s[i][:, part], in_=n2s[i][:, part], func=ACT.Abs_reciprocal_sqrt)
 
-        def at_r(i):
-            if i in RHO_TWICE:
-                nc.vector.tensor_mul(out=qs[i][:], in0=qs[i][:], in1=n2s[i][:])
-            else:
-                nc.scalar.activation(out=n2s[i][:], in_=n2s[i][:], func=ACT.Square)
+        def at_r(i, part=slice(0, KB4)):
+            nc.scalar.activation(out=n2s[i][:, part], in_=n2s[i][:, part], func=ACT.Square)
 
-        def at_f(i):
+        def at_f(i, part=slice(0, PAIRS)):
             fb = fbufs[i % 3]
             spread = fb[:, 0 : PAIRS * (P + G)].rearrange("p (r x) -> p r x", x=P + G)[:, :, 0:P]
-            nc.vector.tensor_mul(out=spread, in0=rk(qs[i]), in1=rk(n2s[i]))
+            nc.vector.tensor_mul(out=spread[:, part], in0=rk(qs[i])[:, part], in1=rk(n2s[i])[:, part])
 
         def at_sum(i):
-            c, a = divmod(i, NT)
             fb = fbufs[i % 3]
-            if a == 0:
-                pulls[c] = side.tile([P, NT, P], F32, name="side")
+            pulls[i] = side.tile([P, P], F32, name="side")
             for r in range(PAIRS + 1):
                 nc.tensor.matmul(
-                    out=pulls[c][:, a, :], lhsT=fb[:, r * P : (r + 1) * P], rhs=ident[:], is_transpose=True,
+                    out=pulls[i][:], lhsT=fb[:, r * P : (r + 1) * P], rhs=ident[:], is_transpose=True,
                     start=(r == 0), stop=(r == PAIRS),
                 )
 
         pls = {}
-
-        def end_copy(c):
-            pls[c] = work.tile([P, CH], F32, name="pl")
-            nc.vector.tensor_scalar(
-                out=pls[c][:], in0=pulls[c][:].rearrange("p a k -> p (a k)"), scalar1=-0.5, scalar2=None, op0=ALU.mult
-            )
-
         c2s = {}
+        outs = {}
 
-        def end_turn(c):
-            c2s[c] = side.tile([P, NT, P], F32, name="side")
-            for a in range(NT):
-                i = c * NT + a
-                nc.tensor.matmul(out=c2s[c][:, a, :], lhsT=pls[c][:, a * P : (a + 1) * P], rhs=backf, is_transpose=True, start=True, stop=False)
-                nc.tensor.matmul(out=c2s[c][:, a, :], lhsT=nc2T[:, i * P : (i + 1) * P], rhs=ident[:], is_transpose=True, start=False, stop=True)
+        def end_copy(i):
+            pls[i] = work.tile([P, P], F32, name="pl")
+            nc.scalar.activation(out=pls[i][:], in_=pulls[i][:], func=ACT.Copy, scale=-0.5)
 
-        def end_out(c):
-            o = work.tile([P, NT, K], F32, name="o")
-            for a in range(NT):
-                i = c * NT + a
-                nc.vector.scalar_tensor_tensor(
-                    out=o[:, a, :], in0=c2s[c][:, a, :], scalar=rs[:, i : i + 1], in1=lgs[c][:, a, :], op0=ALU.mult, op1=ALU.mult
-                )
-            nc.sync.dma_start(
-                out=out[c * CH : (c + 1) * CH, :].rearrange("(p a) k -> p a k", a=NT), in_=o[:]
+        def end_turn(i):
+            c2s[i] = side.tile([P, P], F32, name="side")
+            nc.tensor.matmul(out=c2s[i][:], lhsT=pls[i][:], rhs=backf, is_transpose=True, start=True, stop=False)
+            nc.tensor.matmul(
+                out=c2s[i][:], lhsT=nc2T[:, i * P : (i + 1) * P], rhs=ident[:], is_transpose=True, start=False, stop=True
             )
+
+        def end_out(i):
+            c, a = divmod(i, NT)
+            if a == 0:
+                outs[c] = work.tile([P, NT, K], F32, name="o")
+            nc.vector.scalar_tensor_tensor(
+                out=outs[c][:, a, :], in0=c2s[i][:], scalar=rs[:, i : i + 1], in1=lgs[c][:, a, :],
+                op0=ALU.mult, op1=ALU.mult,
+            )
+            first_tile = {NT - 1: 0} if c < NCH - 1 else {NT - 2: 0, NT - 1: NT - 1}
+            if a in first_tile:
+                tiles = slice(first_tile[a], a + 1)
+                nc.sync.dma_start(
+                    out=out[c * CH : (c + 1) * CH, :].rearrange("(p a) k -> p a k", a=NT)[:, tiles, :],
+                    in_=outs[c][:, tiles, :],
+                )
 
 
         nc.gpsimd.iota(kk[:], pattern=[[1, K]], base=0, channel_multiplier=0, allow_small_or_imprecise_dtypes=True)
-        permute_scales(0, nc.gpsimd)
-        permute_scales(1, nc.gpsimd)
         gpsimd_constants()
+        binomial_start()
+        binomial_ln()
 
         def widen_pair(pr, on_scalar):
             for w in (2 * pr, 2 * pr + 1):
@@ -478,89 +511,82 @@ def tile_attractordepthbinhead_d1p_kernel(
                 turn_x(w // NT, w % NT)
 
         for w in range(NT):
-            widen(0, w, 3)
+            widen(0, w, 2)
             turn_x(0, w)
         for i in range(3):
             nc.vector.tensor_copy(out=vecf[:, i, :], in_=vecs[i][:].rearrange("p h t -> p (h t)"))
-        permute_words(0)
+        permute(0, 0)
+        permute(0, 1)
         for kg in range(2):
             quantize_x(0, kg)
+        permute(0, 2)
+        permute(0, 3)
+        binomial_end()
         for j in range(2 * NCH):
             first(j // 2, j % 2)
             if j == 0:
-                permute_words(1)
-                widen_pair(2, 3)
+                widen_pair(2, 2)
                 turn_pair(2)
+                for t in range(4):
+                    permute(1, t)
+                nc.vector.tensor_mul(out=gw[:], in0=vecf[:, 1, :], in1=vecf[:, 2, :])
             if j == 1:
                 load_x(3)
-            if j in (3, 5):
+                for fb in fbufs:
+                    nc.gpsimd.memset(fb[:], 0.0)
+            if j in (3, 5, 7):
                 second((j - 3) // 2)
             if j >= 1:
                 gain((j - 1) // 2, (j - 1) % 2)
-            if j >= 6:
-                u_out(j - 6)
-            if j == 7:
-                softplus_sum(0)
-            if j % 2 == 1 and j < 7:
+            if j in (1, 3, 5):
                 quantize_x((j + 1) // 2, 0)
             if j + 3 < 2 * NCH:
-                widen_pair(j + 3, 3)
+                widen_pair(j + 3, (3, 4, 4, 4, 4)[j])
                 turn_pair(j + 3)
-            if j % 2 == 1 and j < 7:
+            if j in (1, 3, 5):
                 quantize_x((j + 1) // 2, 1)
+            if j in (3, 5, 7):
+                leave_second((j - 3) // 2)
             if j >= 1:
                 quantize_h((j - 1) // 2, (j - 1) % 2)
-            if j == 1:
-                nc.vector.tensor_mul(out=gw[:], in0=vecf[:, 1, :], in1=vecf[:, 2, :])
-                binomial_start()
-            if j == 5:
-                softplus_abs(0)
-                softplus_abs(1)
-            if j == 6:
-                for b in (0, 1):
-                    softplus_exp(b)
-                for b in (0, 1):
-                    softplus_ln(b)
-                binomial_ln()
-            if j >= 5:
-                u_tile(2 * (j - 5), psum)
-                u_tile(2 * (j - 5) + 1, psum)
-        pair_turn(0)
-        softplus_end(0)
-        softplus_sum(1)
-        pair_consts(0, nc.gpsimd)
-        pair_turn(1)
-        softplus_end(1)
-        second(2)
+                weigh((j - 1) // 2, (j - 1) % 2)
+            if j >= 3:
+                u_turn((j - 3) // 2, (j - 3) % 2)
+            if j in (5, 7):
+                u_out((j - 5) // 2)
+                logits((j - 5) // 2)
         gain(3, 1)
-        u_out(2)
-        binomial_end()
-        pair_consts(1, nc.gpsimd)
-
-        def attract_start(k):
-            at_x(k + 1)
-            at_q(k)
-            at_n(k)
-            at_n2(k)
-            at_xn(k)
-            at_d(k)
-
-        at_x(0)
-        attract_start(0)
         quantize_h(3, 1)
-        second(3)
-        attract_start(1)
-        for c in (2, 3):
-            softplus_abs(c)
-        for c in (2, 3):
+        u_turn(2, 1)
+        u_out(2)
+        logits(2)
+        for c in range(3):
             softplus_exp(c)
-        for c in (2, 3):
+        for c in range(3):
+            softmax_exp(c)
+        second(3)
+        weigh(3, 1)
+        u_turn(3, 0)
+        u_turn(3, 1)
+        leave_second(3)
+        softplus_exp(3)
+        u_out(3)
+        logits(3)
+        softmax_exp(3)
+        softplus_ln(0)
+        softplus_a(0)
+        pair_turn(0)
+        softplus_c(0)
+        pair_copy(0, False)
+        pair_means(0)
+        mean_turn(0)
+        for c in range(1, NCH):
             softplus_ln(c)
-        logits(0)
-        for c in (2, 3):
-            softplus_sum(c)
-        for c in (2, 3):
-            softplus_end(c)
+        mean_copy(0)
+        pair_consts(0)
+        softplus_a(1)
+        pair_turn(1)
+        softmax_end()
 
         def attract_step(k):
             if k + 1 < TILES:
@@ -568,48 +594,59 @@ def tile_attractordepthbinhead_d1p_kernel(
             if k < TILES:
                 at_q(k)
                 at_n(k)
-            if 0 <= k - 3:
+            if 4 <= k:
+                end_copy(k - 4)
+            if 5 <= k:
+                end_out(k - 5)
+            if 3 <= k < TILES + 3:
                 at_f(k - 3)
-            if 0 <= k - 2 < TILES:
+            if 2 <= k < TILES + 2:
                 at_rho(k - 2)
             if k < TILES:
                 at_n2(k)
                 at_xn(k)
                 at_d(k)
-            if 0 <= k - 2 < TILES:
+            if 2 <= k < TILES + 2:
                 at_r(k - 2)
-
-        for k in range(2, TILES + 3):
-            d = k - 4
-            if k == 4:
-                pair_consts(2, nc.gpsimd)
-            if k == 9:
-                pair_consts(3, nc.gpsimd)
-            if d >= 0 and d % NT == NT - 1:
-                end_copy(d // NT)
-            if k in (4, 6, 8, 10, 12):
-                u_out((k + 2) // 2)
-            if k in (5, 9, 13):
-                logits((k - 1) // 4)
-            if k == 16:
-                for c in range(NCH):
-                    softmax_exp(c)
-            attract_step(k)
-            if k >= 3:
+            if 4 <= k:
+                end_turn(k - 4)
+            if 3 <= k < TILES + 3:
                 at_sum(k - 3)
-            if k == 17:
-                softmax_end()
-                end_out(0)
-                end_out(1)
-                end_out(2)
-            if d >= 0 and d % NT == NT - 1:
-                end_turn(d // NT)
-            if k == 2:
-                pair_turn(2)
-            if k == 8:
-                pair_turn(3)
-            if 2 <= k <= 11:
-                u_tile(6 + k - 2)
-        end_copy(3)
-        end_turn(3)
-        end_out(3)
+
+        at_x(0)
+        for k in range(TILES + 1):
+            c, part = divmod(k + 5, 4)
+            ready = c < NCH
+            attract_step(k)
+            if ready and part == 1:
+                pair_copy(c, True)
+                softplus_c(c)
+            if ready and part == 2:
+                pair_means(c)
+                mean_turn(c)
+            if ready and part == 3:
+                mean_copy(c)
+                pair_consts(c)
+            if ready and part == 0:
+                softplus_a(c)
+                pair_turn(c)
+        last = TILES - 1
+        for part in range(2):
+            words = slice(part * 512, (part + 1) * 512)
+            at_rho(last, words)
+            at_r(last, words)
+        end_copy(last - 2)
+        end_out(last - 3)
+        at_f(last - 1)
+        end_turn(last - 2)
+        at_sum(last - 1)
+        for part in range(2):
+            at_f(last, slice(4 * part, 4 * part + 4))
+        end_out(last - 2)
+        end_copy(last - 1)
+        end_turn(last - 1)
+        at_sum(last)
+        end_out(last - 1)
+        end_copy(last)
+        end_turn(last)
+        end_out(last)

@@ -26,7 +26,7 @@ TILES = NCH * NT
 PAIRS = A // 2
 KB4 = 1024
 
-T4_BUFS = 14
+T4_BUFS = 13
 
 FLOPS = 2 * TOK * E * F + 2 * TOK * F * 2 * K + 2 * TOK * F + 12 * TOK * K * A
 
@@ -96,11 +96,12 @@ def tile_attractordepthbinhead_d1p_kernel(
                 out=w1p[:, :, half].rearrange("p k (t m b) -> p k t m b", t=4, b=2)[:, :, t],
                 in_=w1raw[:, :, half].rearrange("p k (m t b) -> p k t m b", t=4, b=2)[:, :, t],
             )
+
+        def permute_scales(hh, eng):
             half = slice(hh * 512, (hh + 1) * 512)
-            eng = nc.vector if hh == 0 else nc.gpsimd
             eng.tensor_copy(
-                out=w1s[:, :, half].rearrange("p k (t m) -> p k t m", t=4)[:, :, t],
-                in_=w1sraw[:, :, half].rearrange("p k (m t) -> p k t m", t=4)[:, :, t],
+                out=w1s[:, :, half].rearrange("p k (t m) -> p k t m", t=4),
+                in_=w1sraw[:, :, half].rearrange("p k (m t) -> p k t m", t=4),
             )
 
         vecf = keep.tile([P, 3, 8], F32, name="vecf")
@@ -140,17 +141,15 @@ def tile_attractordepthbinhead_d1p_kernel(
 
         def turn_x(c, a):
             if a == 0:
-                xgs[c] = [t4("xg0"), t4("xg1")]
+                xgs[c] = work.tile([P, 2, CH, 2], F32, name="xg", align_bytes=64)
             xt = psum.tile([P, 4, P], F32, name="bank")
             words = xss[c, a][:].bitcast(F32)
             for kg in range(2):
                 for u in range(2):
                     nc.tensor.transpose(xt[:, 2 * kg + u, :], words[:, 256 * kg + u : 256 * (kg + 1) : 2], ident[:])
-            for kg in range(2):
-                nc.scalar.copy(
-                    out=xgs[c][kg][:, 2 * a * P : 2 * (a + 1) * P].rearrange("p (r u) -> p r u", u=2),
-                    in_=xt[:, 2 * kg : 2 * kg + 2, :].rearrange("p u r -> p r u"),
-                )
+            nc.scalar.copy(
+                out=xgs[c][:, :, a * P : (a + 1) * P, :], in_=xt[:].rearrange("p (k u) r -> p k r u", u=2)
+            )
 
         xqs = {}
         hqs = {}
@@ -165,7 +164,7 @@ def tile_attractordepthbinhead_d1p_kernel(
             nc.vector.quantize_mx(out=codes[:, kg, :].bitcast(FP8X4), scales=scales[:, kg, :], in_=src)
 
         def quantize_x(c, kg):
-            quantize(c, xqs, kg, xgs[c][kg][:].bitcast(BF16))
+            quantize(c, xqs, kg, xgs[c][:, kg].rearrange("p n u -> p (n u)").bitcast(BF16))
 
         gels = {}
         hbs = {}
@@ -227,7 +226,6 @@ def tile_attractordepthbinhead_d1p_kernel(
         nc2T = keep.tile([P, TOK], F32, name="nc2T")
         sp = {}
         rl = {}
-        dup = {}
 
         def leave_second(c):
             sp[c] = t4("e")
@@ -249,7 +247,7 @@ def tile_attractordepthbinhead_d1p_kernel(
             nc.scalar.activation(out=sp[c][:], in_=sp[c][:], func=ACT.Ln, bias=1.0)
 
         def softplus_a(c):
-            aTs[c] = work.tile([P, CH], F32, name="aT")
+            aTs[c] = work.tile([P, CH], F32, name="aT", bufs=4)
             nc.vector.tensor_add(out=aTs[c][:], in0=rl[c][:, CH:KB4], in1=sp[c][:, CH:KB4])
 
         def softplus_c(c):
@@ -259,59 +257,55 @@ def tile_attractordepthbinhead_d1p_kernel(
             )
 
         tps = {}
-        m2s = {}
+        als = {}
         mps = {}
+        gaps = {}
         m2T = keep.tile([P, TOK], F32, name="m2T")
 
-        def mean_turn(c):
-            mp = side.tile([P, NT, P], F32, name="side")
-            m2f = m2s[c][:].rearrange("p x h j -> p (x h j)")
-            for a in range(NT):
-                nc.tensor.transpose(mp[:, a, :], m2f[:, a * P : (a + 1) * P], ident[:])
-            mps[c] = mp
-
-        def mean_copy(c):
-            nc.scalar.copy(out=m2T[:, c * CH : (c + 1) * CH], in_=mps[c][:].rearrange("p a k -> p (a k)"))
-
         def pair_turn(c):
-            tp = side.tile([P, NT, P], F32, name="side")
-            tps[c] = tp
+            tps[c] = side.tile([P, NT, P], F32, name="side")
             for a in range(NT):
-                nc.tensor.transpose(tp[:, a, :], aTs[c][:, a * P : (a + 1) * P], ident[:])
-
-        als = {}
+                nc.tensor.transpose(tps[c][:, a, :], aTs[c][:, a * P : (a + 1) * P], ident[:])
 
         def pair_copy(c, on_scalar):
-            als[c] = work.tile([P, NT * G, A], F32, name="al")
-            out_, in_ = als[c][:].rearrange("p x i -> p (x i)"), tps[c][:].rearrange("p a k -> p (a k)")
+            als[c] = work.tile([P, NT, A + PAIRS, G], F32, name="al")
+            rows = tps[c][:].rearrange("p a (q i) -> p a i q", i=A)
+            for d in range(2):
+                n = A if d == 0 else PAIRS
+                out_, in_ = als[c][:, :, d * A : d * A + n, :], rows[:, :, 0:n, :]
+                if on_scalar:
+                    nc.scalar.copy(out=out_, in_=in_)
+                else:
+                    nc.vector.tensor_copy(out=out_, in_=in_)
+
+        def mean_turn(c):
+            mps[c] = side.tile([P, NT, P], F32, name="side")
+            for a in range(NT):
+                al = als[c][:, a].rearrange("p i q -> p (i q)")
+                for d in range(2):
+                    nc.tensor.matmul(
+                        out=mps[c][:, a, :], lhsT=al[:, d * PAIRS * G : d * PAIRS * G + P], rhs=ident[:],
+                        is_transpose=True, start=(d == 0), stop=(d == 1),
+                    )
+
+        def mean_copy(c, on_scalar):
+            out_, in_ = m2T[:, c * CH : (c + 1) * CH], mps[c][:].rearrange("p a k -> p (a k)")
             if on_scalar:
                 nc.scalar.copy(out=out_, in_=in_)
             else:
                 nc.vector.tensor_copy(out=out_, in_=in_)
 
-        def pair_means(c):
-            m2s[c] = work.tile([P, NT * G, 2, PAIRS], F32, name="m2", bufs=1)
-            both = [P, NT * G, 2, PAIRS]
-            nc.vector.tensor_add(
-                out=m2s[c][:],
-                in0=als[c][:, :, 0:PAIRS].unsqueeze(2).to_broadcast(both),
-                in1=als[c][:, :, PAIRS:A].unsqueeze(2).to_broadcast(both),
+        def pair_gap(c, on_scalar):
+            gaps[c] = work.tile([P, NT, PAIRS * G], F32, name="gap", bufs=3)
+            al = als[c][:].rearrange("p a i q -> p a (i q)")
+            nc.vector.tensor_sub(
+                out=gaps[c][:], in0=al[:, :, 0 : PAIRS * G], in1=al[:, :, PAIRS * G : 2 * PAIRS * G]
             )
-
-        def pair_consts(c):
-            d2 = work.tile([P, PAIRS, NT * G], F32, name="d2")
-            ai = als[c][:].rearrange("p x i -> p i x")
-            nc.vector.tensor_sub(out=d2[:], in0=ai[:, 0:PAIRS], in1=ai[:, PAIRS:A])
-            d2f = d2[:].rearrange("p j x -> p (j x)")
-            nc.vector.tensor_mul(out=d2f, in0=d2f, in1=d2f)
-            bg = work.tile([P, 2, 2 * PAIRS, NT, G], F32, name="bg", bufs=3)
-            src = d2f.unsqueeze(1).to_broadcast([P, 2, PAIRS * NT * G])
-            for v, (s1, s2) in enumerate(((-1.0, 2.0), (8.0, 0.0))):
-                nc.vector.tensor_scalar(
-                    out=bg[:, v].rearrange("p (h j) a q -> p h (j a q)", h=2), in0=src, scalar1=s1, scalar2=s2,
-                    op0=ALU.mult, op1=ALU.add,
-                )
-            dup[c] = bg
+            flat = gaps[c][:].rearrange("p a j -> p (a j)")
+            if on_scalar:
+                nc.scalar.activation(out=flat, in_=flat, func=ACT.Square)
+            else:
+                nc.vector.tensor_mul(out=flat, in0=flat, in1=flat)
 
         lc = keep.tile([P, K], F32, name="lc")
         lo = keep.tile([P, K], F32, name="lo")
@@ -337,6 +331,9 @@ def tile_attractordepthbinhead_d1p_kernel(
             nc.vector.tensor_scalar(
                 out=lc[:], in0=l1[:], scalar1=-1.0, scalar2=n * math.log(n), op0=ALU.mult, op1=ALU.add
             )
+
+        def binomial_exp():
+            nc.scalar.activation(out=lc[:], in_=lc[:], func=ACT.Exp, scale=1.0 / 20.0)
 
         us = keep.tile([P, TILES], F32, name="us")
         ssum = keep.tile([P, TILES], F32, name="ssum")
@@ -366,21 +363,27 @@ def tile_attractordepthbinhead_d1p_kernel(
         def u_out(c):
             nc.vector.tensor_reduce(out=us[:, c * NT : (c + 1) * NT], in_=uts[c][:], axis=AX.X, op=ALU.add)
 
-        def logits(c):
-            for a in range(NT):
-                i = c * NT + a
-                nc.vector.scalar_tensor_tensor(
-                    out=lgs[c][:, a, :], in0=kk[:], scalar=us[:, i : i + 1], in1=lc[:], op0=ALU.mult, op1=ALU.add
-                )
+        def exponents(c):
             cols = slice(c * NT, (c + 1) * NT)
-            nc.vector.tensor_reduce(out=mx[:, cols], in_=lgs[c][:], axis=AX.X, op=ALU.max)
-            nc.vector.tensor_scalar(out=mx[:, cols], in0=mx[:, cols], scalar1=-1.0 / 20.0, scalar2=None, op0=ALU.mult)
+            nc.vector.tensor_scalar(
+                out=us[:, cols], in0=us[:, cols], scalar1=1.0 / 20.0, scalar2=None, op0=ALU.mult
+            )
+            nc.vector.tensor_scalar(
+                out=mx[:, cols], in0=us[:, cols], scalar1=1.0 - K, scalar2=0.0, op0=ALU.mult, op1=ALU.min
+            )
 
         def softmax_exp(c):
             for a in range(NT):
                 i = c * NT + a
                 nc.scalar.activation(
-                    out=lgs[c][:, a, :], in_=lgs[c][:, a, :], func=ACT.Exp, bias=mx[:, i : i + 1], scale=1.0 / 20.0,
+                    out=lgs[c][:, a, :], in_=kk[:], func=ACT.Exp, bias=mx[:, i : i + 1], scale=us[:, i : i + 1]
+                )
+
+        def softmax_sum(c):
+            for a in range(NT):
+                i = c * NT + a
+                nc.vector.scalar_tensor_tensor(
+                    out=lgs[c][:, a, :], in0=lgs[c][:, a, :], scalar=1.0, in1=lc[:], op0=ALU.mult, op1=ALU.mult,
                     accum_out=ssum[:, i : i + 1],
                 )
 
@@ -401,10 +404,10 @@ def tile_attractordepthbinhead_d1p_kernel(
                 xp = psum.tile([P, 4, P], F32, name="bank")
                 xps[i].append(xp)
                 for rr in range(4):
-                    terms = ((m2T, 0), (nc2T, 4 * b + rr))
-                    for k, (src, turn) in enumerate(terms):
+                    terms = ((m2T, ident[:]), (nc2T, turned(4 * b + rr)))
+                    for k, (src, moving) in enumerate(terms):
                         nc.tensor.matmul(
-                            out=xp[:, rr, :], lhsT=src[:, ts], rhs=turned(turn), is_transpose=True,
+                            out=xp[:, rr, :], lhsT=src[:, ts], rhs=moving, is_transpose=True,
                             start=(k == 0), stop=(k == 1),
                         )
 
@@ -415,21 +418,22 @@ def tile_attractordepthbinhead_d1p_kernel(
                     out=qs[i][:, b * 512 : (b + 1) * 512], in_=xps[i][b][:].rearrange("p r k -> p (r k)"), func=ACT.Square
                 )
 
-        def row(i, v):
+        def gap_row(i, n):
             c, a = divmod(i, NT)
-            return dup[c][:, v, :, a, :].unsqueeze(1).to_broadcast([P, PAIRS, A, G])
+            return gaps[c][:, a].unsqueeze(1).to_broadcast([P, n, PAIRS * G])
+
+        def by_gap(t):
+            return t.rearrange("p (r j) -> p r j", j=PAIRS * G)
 
         def rk(t):
-            return t[:].rearrange("p (r k) -> p r k", k=P)
-
-        def rsq(t):
-            return t[:].rearrange("p (r s q) -> p r s q", s=A, q=G)
+            return t.rearrange("p (r k) -> p r k", k=P)
 
         def at_n(i):
             ns[i] = t4("n")
-            for b in range(2):
-                half = slice(b * PAIRS // 2, (b + 1) * PAIRS // 2)
-                nc.vector.tensor_add(out=rsq(ns[i])[:, half], in0=rsq(qs[i])[:, half], in1=row(i, 0)[:, half])
+            nc.vector.scalar_tensor_tensor(
+                out=by_gap(ns[i][:]), in0=by_gap(qs[i][:]), scalar=2.0, in1=gap_row(i, KB4 // 64),
+                op0=ALU.add, op1=ALU.subtract,
+            )
 
         def at_n2(i):
             n2s[i] = t4("n2")
@@ -442,8 +446,12 @@ def tile_attractordepthbinhead_d1p_kernel(
                     out=qs[i][:, half], in0=xps[i][b][:].rearrange("p r k -> p (r k)"), in1=ns[i][:, half]
                 )
 
-        def at_d(i):
-            nc.vector.tensor_add(out=rsq(n2s[i]), in0=rsq(n2s[i]), in1=row(i, 1))
+        def at_d(i, part=slice(0, KB4)):
+            cols = by_gap(n2s[i][:, part])
+            nc.vector.scalar_tensor_tensor(
+                out=cols, in0=gap_row(i, (part.stop - part.start) // 64), scalar=8.0, in1=cols,
+                op0=ALU.mult, op1=ALU.add,
+            )
 
         def at_rho(i, part=slice(0, KB4)):
             nc.scalar.activation(out=n2s[i][:, part], in_=n2s[i][:, part], func=ACT.Abs_reciprocal_sqrt)
@@ -454,7 +462,7 @@ def tile_attractordepthbinhead_d1p_kernel(
         def at_f(i, part=slice(0, PAIRS)):
             fb = fbufs[i % 3]
             spread = fb[:, 0 : PAIRS * (P + G)].rearrange("p (r x) -> p r x", x=P + G)[:, :, 0:P]
-            nc.vector.tensor_mul(out=spread[:, part], in0=rk(qs[i])[:, part], in1=rk(n2s[i])[:, part])
+            nc.vector.tensor_mul(out=spread[:, part], in0=rk(qs[i][:])[:, part], in1=rk(n2s[i][:])[:, part])
 
         def at_sum(i):
             fb = fbufs[i % 3]
@@ -499,6 +507,9 @@ def tile_attractordepthbinhead_d1p_kernel(
 
         nc.gpsimd.iota(kk[:], pattern=[[1, K]], base=0, channel_multiplier=0, allow_small_or_imprecise_dtypes=True)
         gpsimd_constants()
+        permute_scales(1, nc.gpsimd)
+        for fb in fbufs:
+            nc.gpsimd.memset(fb[:], 0.0)
         binomial_start()
         binomial_ln()
 
@@ -510,12 +521,15 @@ def tile_attractordepthbinhead_d1p_kernel(
             for w in (2 * pr, 2 * pr + 1):
                 turn_x(w // NT, w % NT)
 
-        for w in range(NT):
+        widen(0, 0, 2)
+        for w in range(1, NT):
             widen(0, w, 2)
-            turn_x(0, w)
+            turn_x(0, w - 1)
+        turn_x(0, NT - 1)
         for i in range(3):
             nc.vector.tensor_copy(out=vecf[:, i, :], in_=vecs[i][:].rearrange("p h t -> p (h t)"))
         permute(0, 0)
+        permute_scales(0, nc.vector)
         permute(0, 1)
         for kg in range(2):
             quantize_x(0, kg)
@@ -532,8 +546,6 @@ def tile_attractordepthbinhead_d1p_kernel(
                 nc.vector.tensor_mul(out=gw[:], in0=vecf[:, 1, :], in1=vecf[:, 2, :])
             if j == 1:
                 load_x(3)
-                for fb in fbufs:
-                    nc.gpsimd.memset(fb[:], 0.0)
             if j in (3, 5, 7):
                 second((j - 3) // 2)
             if j >= 1:
@@ -541,7 +553,7 @@ def tile_attractordepthbinhead_d1p_kernel(
             if j in (1, 3, 5):
                 quantize_x((j + 1) // 2, 0)
             if j + 3 < 2 * NCH:
-                widen_pair(j + 3, (3, 4, 4, 4, 4)[j])
+                widen_pair(j + 3, (3, 3, 3, 3, 3)[j])
                 turn_pair(j + 3)
             if j in (1, 3, 5):
                 quantize_x((j + 1) // 2, 1)
@@ -549,63 +561,75 @@ def tile_attractordepthbinhead_d1p_kernel(
                 leave_second((j - 3) // 2)
             if j >= 1:
                 quantize_h((j - 1) // 2, (j - 1) % 2)
+            if j == 7:
+                gain(3, 1)
+            if j >= 1:
                 weigh((j - 1) // 2, (j - 1) % 2)
             if j >= 3:
                 u_turn((j - 3) // 2, (j - 3) % 2)
-            if j in (5, 7):
-                u_out((j - 5) // 2)
-                logits((j - 5) // 2)
-        gain(3, 1)
+            if j == 5:
+                u_out(0)
+                exponents(0)
         quantize_h(3, 1)
         u_turn(2, 1)
-        u_out(2)
-        logits(2)
-        for c in range(3):
-            softplus_exp(c)
-        for c in range(3):
-            softmax_exp(c)
         second(3)
         weigh(3, 1)
         u_turn(3, 0)
         u_turn(3, 1)
+        for c in range(3):
+            softplus_exp(c)
         leave_second(3)
         softplus_exp(3)
-        u_out(3)
-        logits(3)
-        softmax_exp(3)
-        softplus_ln(0)
+        u_out(1)
+        exponents(1)
+        u_out(2)
+        exponents(2)
+        for c in range(NCH):
+            softplus_ln(c)
         softplus_a(0)
         pair_turn(0)
         softplus_c(0)
         pair_copy(0, False)
-        pair_means(0)
         mean_turn(0)
-        for c in range(1, NCH):
-            softplus_ln(c)
-        mean_copy(0)
-        pair_consts(0)
+        pair_gap(0, False)
+        u_out(3)
+        exponents(3)
+        mean_copy(0, False)
+        at_x(0)
         softplus_a(1)
         pair_turn(1)
-        softmax_end()
+        softplus_c(1)
+        for c in (2, 3):
+            softplus_a(c)
+            softplus_c(c)
+        binomial_exp()
+        for c in range(NCH - 1):
+            softmax_exp(c)
+        at_q(0)
+        softmax_exp(NCH - 1)
+        pair_copy(1, True)
 
         def attract_step(k):
             if k + 1 < TILES:
-                at_x(k + 1)
-            if k < TILES:
-                at_q(k)
-                at_n(k)
+                at_q(k + 1)
             if 4 <= k:
                 end_copy(k - 4)
+            if k < TILES:
+                at_n(k)
             if 5 <= k:
                 end_out(k - 5)
+            if k < TILES:
+                at_xn(k)
+            if k + 2 < TILES:
+                at_x(k + 2)
             if 3 <= k < TILES + 3:
                 at_f(k - 3)
             if 2 <= k < TILES + 2:
                 at_rho(k - 2)
+            if 1 <= k < TILES:
+                at_d(k - 1)
             if k < TILES:
                 at_n2(k)
-                at_xn(k)
-                at_d(k)
             if 2 <= k < TILES + 2:
                 at_r(k - 2)
             if 4 <= k:
@@ -613,40 +637,49 @@ def tile_attractordepthbinhead_d1p_kernel(
             if 3 <= k < TILES + 3:
                 at_sum(k - 3)
 
-        at_x(0)
-        for k in range(TILES + 1):
-            c, part = divmod(k + 5, 4)
-            ready = c < NCH
+        at_x(1)
+        for k in range(TILES):
+            c, part = divmod(k + 6, 4)
             attract_step(k)
-            if ready and part == 1:
-                pair_copy(c, True)
-                softplus_c(c)
-            if ready and part == 2:
-                pair_means(c)
-                mean_turn(c)
-            if ready and part == 3:
-                mean_copy(c)
-                pair_consts(c)
-            if ready and part == 0:
-                softplus_a(c)
-                pair_turn(c)
+            if k < NCH:
+                softmax_sum(k)
+            if k == NCH - 1:
+                softmax_end()
+            if c < NCH:
+                if part == 0:
+                    pair_turn(c)
+                elif part == 1:
+                    pair_copy(c, True)
+                elif part == 2:
+                    mean_turn(c)
+                    pair_gap(c, True)
+                else:
+                    mean_copy(c, True)
+
         last = TILES - 1
-        for part in range(2):
-            words = slice(part * 512, (part + 1) * 512)
-            at_rho(last, words)
-            at_r(last, words)
-        end_copy(last - 2)
-        end_out(last - 3)
+        halves = [slice(0, 512), slice(512, 1024)]
+        at_rho(last - 1)
+        for part in halves:
+            at_d(last, part)
+        end_copy(last - 3)
+        at_f(last - 2)
+        at_r(last - 1)
+        end_turn(last - 3)
+        at_sum(last - 2)
+        end_out(last - 4)
+        for part in halves:
+            at_rho(last, part)
+            at_r(last, part)
         at_f(last - 1)
+        end_out(last - 3)
+        end_copy(last - 2)
         end_turn(last - 2)
         at_sum(last - 1)
         for part in range(2):
             at_f(last, slice(4 * part, 4 * part + 4))
-        end_out(last - 2)
-        end_copy(last - 1)
-        end_turn(last - 1)
         at_sum(last)
-        end_out(last - 1)
-        end_copy(last)
-        end_turn(last)
-        end_out(last)
+        end_out(last - 2)
+        for i in (last - 1, last):
+            end_copy(i)
+            end_turn(i)
+            end_out(i)

@@ -104,6 +104,7 @@ def tile_attractordepthbinhead_d1p_kernel(
                 in_=w1sraw[:, :, half].rearrange("p k (m t) -> p k t m", t=4),
             )
 
+        warm = keep.tile([P, 1], F32, name="warm")
         vecf = keep.tile([P, 3, 8], F32, name="vecf")
         gw = keep.tile([P, 8], F32, name="gw")
 
@@ -116,10 +117,10 @@ def tile_attractordepthbinhead_d1p_kernel(
 
         def gpsimd_constants():
             for d in range(2):
-                nc.gpsimd.tensor_copy(
+                nc.vector.tensor_copy(
                     out=rot[:, d * A : (d + 1) * A, :], in_=ident[:].rearrange("p (q i) -> p i q", i=A)
                 )
-            nc.gpsimd.tensor_copy(out=back[:], in_=ident[:].rearrange("p (i q) -> p q i", i=A))
+            nc.vector.tensor_copy(out=back[:], in_=ident[:].rearrange("p (i q) -> p q i", i=A))
 
         def turned(r):
             return rotf[:, r * G : r * G + P]
@@ -505,13 +506,14 @@ def tile_attractordepthbinhead_d1p_kernel(
                 )
 
 
-        nc.gpsimd.iota(kk[:], pattern=[[1, K]], base=0, channel_multiplier=0, allow_small_or_imprecise_dtypes=True)
+        nc.gpsimd.memset(warm[:], 0.0)
+        nc.scalar.activation(out=warm[:], in_=warm[:], func=ACT.Gelu)
         gpsimd_constants()
-        permute_scales(1, nc.gpsimd)
+        nc.gpsimd.iota(kk[:], pattern=[[1, K]], base=0, channel_multiplier=0, allow_small_or_imprecise_dtypes=True)
         for fb in fbufs:
-            nc.gpsimd.memset(fb[:], 0.0)
-        binomial_start()
-        binomial_ln()
+            rows = fb[:, 0 : PAIRS * (P + G)].rearrange("p (r x) -> p r x", x=P + G)
+            nc.gpsimd.memset(rows[:, :, P : P + G], 0.0)
+            nc.gpsimd.memset(fb[:, PAIRS * (P + G) : 9 * P], 0.0)
 
         def widen_pair(pr, on_scalar):
             for w in (2 * pr, 2 * pr + 1):
@@ -535,7 +537,6 @@ def tile_attractordepthbinhead_d1p_kernel(
             quantize_x(0, kg)
         permute(0, 2)
         permute(0, 3)
-        binomial_end()
         for j in range(2 * NCH):
             first(j // 2, j % 2)
             if j == 0:
@@ -543,11 +544,15 @@ def tile_attractordepthbinhead_d1p_kernel(
                 turn_pair(2)
                 for t in range(4):
                     permute(1, t)
+                permute_scales(1, nc.vector)
                 nc.vector.tensor_mul(out=gw[:], in0=vecf[:, 1, :], in1=vecf[:, 2, :])
+                binomial_start()
             if j == 1:
                 load_x(3)
             if j in (3, 5, 7):
                 second((j - 3) // 2)
+            if j >= 4:
+                u_turn((j - 4) // 2, (j - 4) % 2)
             if j >= 1:
                 gain((j - 1) // 2, (j - 1) % 2)
             if j in (1, 3, 5):
@@ -559,20 +564,21 @@ def tile_attractordepthbinhead_d1p_kernel(
                 quantize_x((j + 1) // 2, 1)
             if j in (3, 5, 7):
                 leave_second((j - 3) // 2)
+            if j >= 6:
+                weigh((j - 1) // 2, (j - 1) % 2)
             if j >= 1:
                 quantize_h((j - 1) // 2, (j - 1) % 2)
             if j == 7:
                 gain(3, 1)
-            if j >= 1:
+            if 1 <= j < 6:
                 weigh((j - 1) // 2, (j - 1) % 2)
-            if j >= 3:
-                u_turn((j - 3) // 2, (j - 3) % 2)
-            if j == 5:
+            if j == 6:
                 u_out(0)
                 exponents(0)
         quantize_h(3, 1)
-        u_turn(2, 1)
         second(3)
+        u_turn(2, 0)
+        u_turn(2, 1)
         weigh(3, 1)
         u_turn(3, 0)
         u_turn(3, 1)
@@ -586,12 +592,14 @@ def tile_attractordepthbinhead_d1p_kernel(
         exponents(2)
         for c in range(NCH):
             softplus_ln(c)
+        binomial_ln()
         softplus_a(0)
         pair_turn(0)
         softplus_c(0)
         pair_copy(0, False)
         mean_turn(0)
         pair_gap(0, False)
+        binomial_end()
         u_out(3)
         exponents(3)
         mean_copy(0, False)
@@ -602,11 +610,11 @@ def tile_attractordepthbinhead_d1p_kernel(
         for c in (2, 3):
             softplus_a(c)
             softplus_c(c)
-        binomial_exp()
         for c in range(NCH - 1):
             softmax_exp(c)
         at_q(0)
         softmax_exp(NCH - 1)
+        binomial_exp()
         pair_copy(1, True)
 
         def attract_step(k):

import math
from contextlib import ExitStack

import concourse.mybir as mybir
from concourse.masks import make_identity

F32 = mybir.dt.float32
BF16 = mybir.dt.bfloat16
I32 = mybir.dt.int32
U32 = mybir.dt.uint32
U8 = mybir.dt.uint8
E4M3 = mybir.dt.float8_e4m3fn
FP8X4 = mybir.dt.float8_e4m3fn_x4
FP4X4 = mybir.dt.float4_e2m1fn_x4
ALU = mybir.AluOpType
ACT = mybir.ActivationFunctionType
AX = mybir.AxisListType

P = 128
TOK, E, F, G, A = 2048, 1024, 1024, 8, 16
K = G * A
CH = 512
NCH = TOK // CH
NT = CH // P
TILES = NCH * NT
PAIRS = A // 2
KB4 = 1024

T4_BUFS = 13

FLOPS = 2 * TOK * E * F + 2 * TOK * F * 2 * K + 2 * TOK * F + 12 * TOK * K * A


def tile_attractordepthbinhead_d1p_kernel(
    tc, x_bytes, x_scale, w1_words, w1_scales, b1, g, w_head_words, w_head_scales, w_q, out
):
    nc = tc.nc
    with ExitStack() as ctx:
        keep = ctx.enter_context(tc.tile_pool(name="keep", bufs=1))
        work = ctx.enter_context(tc.tile_pool(name="work", bufs=2))
        psum = ctx.enter_context(tc.psum_pool(name="psum", bufs=5))
        side = ctx.enter_context(tc.psum_pool(name="side", bufs=3))
        ctx.enter_context(tc.manual_schedule())

        def t4(name):
            return work.tile([P, KB4], F32, name=name, tag="t4", bufs=T4_BUFS, align_bytes=64)

        xsc = keep.tile([P, NCH, NT, 8], F32, name="xsc")
        nc.scalar.dma_start(out=xsc[:], in_=x_scale.rearrange("(c p a) j -> p c a j", p=P, a=NT))
        vecs = []
        for i, v in enumerate((b1, g, w_q)):
            vec = keep.tile([P, 2, 4], BF16, name="vec%d" % i)
            nc.scalar.dma_start(out=vec[:], in_=v.rearrange("(h p t) -> p h t", h=2, t=4))
            vecs.append(vec)

        w1raw = keep.tile([P, 2, 2 * F], U8, name="w1raw")
        w1sraw = keep.tile([P, 2, F], U8, name="w1sraw", align_bytes=64)
        wh = keep.tile([P, 2, 4 * K], U8, name="wh", align_bytes=64)
        whs = keep.tile([P, 2, 2 * K], U8, name="whs", align_bytes=64)
        nc.vector.memset(w1sraw[:].rearrange("p h n -> p (h n)").bitcast(I32), 0)
        nc.gpsimd.memset(whs[:].rearrange("p h n -> p (h n)").bitcast(I32), 0)

        xbs = {}

        def load_x(c, pieces=1):
            xb = work.tile([P, NT, E], U8, name="xb", bufs=3)
            xbs[c] = xb
            src = x_bytes[c * CH : (c + 1) * CH, :].rearrange("(p a) k -> p a k", a=NT)
            n = NT // pieces
            for i in range(pieces):
                nc.sync.dma_start(out=xb[:, i * n : (i + 1) * n, :], in_=src[:, i * n : (i + 1) * n, :])

        def load_scales(dst, src):
            for h in range(2):
                for q in range(4):
                    nc.sync.dma_start(
                        out=dst[32 * q : 32 * q + 4, h, :].bitcast(I32), in_=src[h, 4 * q : 4 * q + 4, :].bitcast(I32)
                    )

        load_x(0, 2)
        nc.sync.dma_start(out=w1raw[:], in_=w1_words.rearrange("h p n -> p h n"))
        load_scales(w1sraw, w1_scales)
        load_x(1)
        nc.sync.dma_start(out=wh[:], in_=w_head_words.rearrange("h p n -> p h n"))
        load_scales(whs, w_head_scales)
        load_x(2)

        ident = keep.tile([P, P], F32, name="ident")
        make_identity(nc, ident[:])
        w1p = keep.tile([P, 2, 2 * F], U8, name="w1p", align_bytes=64)
        w1s = keep.tile([P, 2, F], U8, name="w1s", align_bytes=64)

        def permute(hh, t):
            half = slice(hh * F, (hh + 1) * F)
            nc.vector.tensor_copy(
                out=w1p[:, :, half].rearrange("p k (t m b) -> p k t m b", t=4, b=2)[:, :, t],
                in_=w1raw[:, :, half].rearrange("p k (m t b) -> p k t m b", t=4, b=2)[:, :, t],
            )

        def permute_scales(hh, eng):
            half = slice(hh * 512, (hh + 1) * 512)
            eng.tensor_copy(
                out=w1s[:, :, half].rearrange("p k (t m) -> p k t m", t=4),
                in_=w1sraw[:, :, half].rearrange("p k (m t) -> p k t m", t=4),
            )

        warm = keep.tile([P, 1], F32, name="warm")
        vecf = keep.tile([P, 3, 8], F32, name="vecf")
        gw = keep.tile([P, 8], F32, name="gw")

        rot = keep.tile([P, 2 * A, G], F32, name="rot")
        back = keep.tile([P, G, A], F32, name="back")
        rotf = rot[:].rearrange("p i q -> p (i q)")
        backf = back[:].rearrange("p q i -> p (q i)")
        fbufs = [keep.tile([P, 9 * P], F32, name="fb%d" % i) for i in range(3)]
        kk = keep.tile([P, K], F32, name="kk")

        def gpsimd_constants():
            for d in range(2):
                nc.vector.tensor_copy(
                    out=rot[:, d * A : (d + 1) * A, :], in_=ident[:].rearrange("p (q i) -> p i q", i=A)
                )
            nc.vector.tensor_copy(out=back[:], in_=ident[:].rearrange("p (i q) -> p q i", i=A))

        def turned(r):
            return rotf[:, r * G : r * G + P]

        xgs = {}
        xss = {}

        def widen(c, a, on_scalar):
            xs = work.tile([P, E], BF16, name="xs", bufs=4)
            xss[c, a] = xs
            for j in range(8):
                src = xbs[c][:, a, j * P : (j + 1) * P].bitcast(E4M3)
                sc = xsc[:, c, a, j : j + 1]
                dst = xs[:, j * P : (j + 1) * P]
                if j >= 8 - on_scalar:
                    nc.scalar.activation(out=dst, in_=src, func=ACT.Copy, scale=sc)
                else:
                    nc.vector.tensor_scalar(out=dst, in0=src, scalar1=sc, scalar2=None, op0=ALU.mult)

        def turn_x(c, a):
            if a == 0:
                xgs[c] = work.tile([P, 2, CH, 2], F32, name="xg", align_bytes=64)
            xt = psum.tile([P, 4, P], F32, name="bank")
            words = xss[c, a][:].bitcast(F32)
            for kg in range(2):
                for u in range(2):
                    nc.tensor.transpose(xt[:, 2 * kg + u, :], words[:, 256 * kg + u : 256 * (kg + 1) : 2], ident[:])
            nc.scalar.copy(
                out=xgs[c][:, :, a * P : (a + 1) * P, :], in_=xt[:].rearrange("p (k u) r -> p k r u", u=2)
            )

        xqs = {}
        hqs = {}

        def quantize(key, store, kg, src):
            if kg == 0:
                store[key] = (
                    work.tile([P, 2, CH], U32, name="codes", bufs=4, align_bytes=64),
                    work.tile([P, 2, CH], U8, name="scales", bufs=4, align_bytes=64),
                )
            codes, scales = store[key]
            nc.vector.quantize_mx(out=codes[:, kg, :].bitcast(FP8X4), scales=scales[:, kg, :], in_=src)

        def quantize_x(c, kg):
            quantize(c, xqs, kg, xgs[c][:, kg].rearrange("p n u -> p (n u)").bitcast(BF16))

        gels = {}
        hbs = {}

        def first(c, hh):
            gel = work.tile([P, 4, CH], F32, name="gel", bufs=6)
            gels[c, hh] = gel
            codes, scales = xqs[c]
            for t in range(4):
                ps = psum.tile([P, CH], F32, name="bank")
                for kg in range(2):
                    b0 = hh * F + t * 2 * P
                    s0 = hh * 512 + t * P
                    nc.tensor.matmul_mx(
                        out=ps[:],
                        lhsT=w1p[:, kg, b0 : b0 + 2 * P].bitcast(FP4X4),
                        lhsT_scale=w1s[:, kg, s0 : s0 + P],
                        rhs=codes[:, kg, :].bitcast(FP8X4),
                        rhs_scale=scales[:, kg, :],
                        start=(kg == 0),
                        stop=(kg == 1),
                    )
                nc.scalar.activation(
                    out=gel[:, t, :], in_=ps[:], func=ACT.Gelu, bias=vecf[:, 0, 4 * hh + t : 4 * hh + t + 1]
                )

        def gain(c, hh):
            hb = t4("hb")
            hbs[c, hh] = hb
            nc.vector.tensor_tensor(
                out=hb[:].bitcast(BF16).rearrange("p (n t) -> p n t", t=4),
                in0=gels[c, hh][:].rearrange("p t n -> p n t"),
                in1=vecf[:, 1, 4 * hh : 4 * hh + 4].unsqueeze(1).to_broadcast([P, CH, 4]),
                op=ALU.mult,
            )

        def quantize_h(c, hh):
            quantize(c, hqs, hh, hbs[c, hh][:].bitcast(BF16))

        yps = {}

        def second(c):
            codes, scales = hqs[c]
            for s in range(2):
                y = side.tile([P, CH], F32, name="side")
                yps[c, s] = y
                for hh in range(2):
                    nc.tensor.matmul_mx(
                        out=y[:],
                        lhsT=wh[:, hh, s * 2 * P : (s + 1) * 2 * P].bitcast(FP4X4),
                        lhsT_scale=whs[:, hh, s * P : (s + 1) * P],
                        rhs=codes[:, hh, :].bitcast(FP8X4),
                        rhs_scale=scales[:, hh, :],
                        start=(hh == 0),
                        stop=(hh == 1),
                    )

        aTs = {}
        nc2T = keep.tile([P, TOK], F32, name="nc2T")
        sp = {}
        rl = {}

        def leave_second(c):
            sp[c] = t4("e")
            rl[c] = t4("rl")
            for s in range(2):
                half = slice(s * CH, (s + 1) * CH)
                nc.scalar.activation(out=sp[c][:, half], in_=yps[c, s][:], func=ACT.Abs)
                if c < NCH - 1:
                    nc.scalar.activation(out=rl[c][:, half], in_=yps[c, s][:], func=ACT.Relu, scale=2.0 - s)
                else:
                    nc.vector.tensor_scalar(
                        out=rl[c][:, half], in0=yps[c, s][:], scalar1=0.0, scalar2=2.0 - s, op0=ALU.max, op1=ALU.mult
                    )

        def softplus_exp(c):
            nc.scalar.activation(out=sp[c][:], in_=sp[c][:], func=ACT.Exp, scale=-1.0)

        def softplus_ln(c):
            nc.scalar.activation(out=sp[c][:], in_=sp[c][:], func=ACT.Ln, bias=1.0)

        def softplus_a(c):
            aTs[c] = work.tile([P, CH], F32, name="aT", bufs=4)
            nc.vector.tensor_add(out=aTs[c][:], in0=rl[c][:, CH:KB4], in1=sp[c][:, CH:KB4])

        def softplus_c(c):
            nc.vector.scalar_tensor_tensor(
                out=nc2T[:, c * CH : (c + 1) * CH], in0=sp[c][:, 0:CH], scalar=-2.0, in1=rl[c][:, 0:CH],
                op0=ALU.mult, op1=ALU.subtract,
            )

        tps = {}
        als = {}
        mps = {}
        gaps = {}
        m2T = keep.tile([P, TOK], F32, name="m2T")

        def pair_turn(c):
            tps[c] = side.tile([P, NT, P], F32, name="side")
            for a in range(NT):
                nc.tensor.transpose(tps[c][:, a, :], aTs[c][:, a * P : (a + 1) * P], ident[:])

        def pair_copy(c, on_scalar):
            als[c] = work.tile([P, NT, A + PAIRS, G], F32, name="al")
            rows = tps[c][:].rearrange("p a (q i) -> p a i q", i=A)
            for d in range(2):
                n = A if d == 0 else PAIRS
                out_, in_ = als[c][:, :, d * A : d * A + n, :], rows[:, :, 0:n, :]
                if on_scalar:
                    nc.scalar.copy(out=out_, in_=in_)
                else:
                    nc.vector.tensor_copy(out=out_, in_=in_)

        def mean_turn(c):
            mps[c] = side.tile([P, NT, P], F32, name="side")
            for a in range(NT):
                al = als[c][:, a].rearrange("p i q -> p (i q)")
                for d in range(2):
                    nc.tensor.matmul(
                        out=mps[c][:, a, :], lhsT=al[:, d * PAIRS * G : d * PAIRS * G + P], rhs=ident[:],
                        is_transpose=True, start=(d == 0), stop=(d == 1),
                    )

        def mean_copy(c, on_scalar):
            out_, in_ = m2T[:, c * CH : (c + 1) * CH], mps[c][:].rearrange("p a k -> p (a k)")
            if on_scalar:
                nc.scalar.copy(out=out_, in_=in_)
            else:
                nc.vector.tensor_copy(out=out_, in_=in_)

        def pair_gap(c, on_scalar):
            gaps[c] = work.tile([P, NT, PAIRS * G], F32, name="gap", bufs=3)
            al = als[c][:].rearrange("p a i q -> p a (i q)")
            nc.vector.tensor_sub(
                out=gaps[c][:], in0=al[:, :, 0 : PAIRS * G], in1=al[:, :, PAIRS * G : 2 * PAIRS * G]
            )
            flat = gaps[c][:].rearrange("p a j -> p (a j)")
            if on_scalar:
                nc.scalar.activation(out=flat, in_=flat, func=ACT.Square)
            else:
                nc.vector.tensor_mul(out=flat, in0=flat, in1=flat)

        lc = keep.tile([P, K], F32, name="lc")
        lo = keep.tile([P, K], F32, name="lo")
        up = keep.tile([P, K], F32, name="up")
        l1 = keep.tile([P, K], F32, name="l1")
        l2 = keep.tile([P, K], F32, name="l2")

        def binomial_start():
            n = float(K - 1)
            nc.vector.tensor_scalar(out=lo[:], in0=kk[:], scalar1=1e-6, scalar2=None, op0=ALU.add)
            nc.vector.tensor_scalar(out=up[:], in0=kk[:], scalar1=-1.0, scalar2=n, op0=ALU.mult, op1=ALU.add)
            nc.vector.tensor_scalar(out=up[:], in0=up[:], scalar1=1e-6, scalar2=None, op0=ALU.add)

        def binomial_ln():
            nc.scalar.activation(out=l1[:], in_=lo[:], func=ACT.Ln)
            nc.scalar.activation(out=l2[:], in_=up[:], func=ACT.Ln)

        def binomial_end():
            n = float(K - 1)
            nc.vector.tensor_mul(out=l1[:], in0=l1[:], in1=lo[:])
            nc.vector.tensor_mul(out=l2[:], in0=l2[:], in1=up[:])
            nc.vector.tensor_add(out=l1[:], in0=l1[:], in1=l2[:])
            nc.vector.tensor_scalar(
                out=lc[:], in0=l1[:], scalar1=-1.0, scalar2=n * math.log(n), op0=ALU.mult, op1=ALU.add
            )

        def binomial_exp():
            nc.scalar.activation(out=lc[:], in_=lc[:], func=ACT.Exp, scale=1.0 / 20.0)

        us = keep.tile([P, TILES], F32, name="us")
        ssum = keep.tile([P, TILES], F32, name="ssum")
        rs = keep.tile([P, TILES], F32, name="rs")
        mx = keep.tile([P, TILES], F32, name="mx")
        lgs = [keep.tile([P, NT, K], F32, name="lg%d" % c) for c in range(NCH)]
        uts = {}

        def weigh(c, hh):
            gel = gels[c, hh]
            for t in range(4):
                m = 4 * hh + t
                nc.vector.tensor_scalar(
                    out=gel[:, t, :], in0=gel[:, t, :], scalar1=gw[:, m : m + 1], scalar2=None, op0=ALU.mult
                )

        def u_turn(c, part):
            if part == 0:
                uts[c] = psum.tile([P, NT, P], F32, name="bank")
            for a in (2 * part, 2 * part + 1):
                for m in range(8):
                    nc.tensor.matmul(
                        out=uts[c][:, a, :], lhsT=gels[c, m // 4][:, m % 4, a * P : (a + 1) * P], rhs=ident[:],
                        is_transpose=True, start=(m == 0), stop=(m == 7),
                    )

        def u_out(c):
            nc.vector.tensor_reduce(out=us[:, c * NT : (c + 1) * NT], in_=uts[c][:], axis=AX.X, op=ALU.add)

        def exponents(c):
            cols = slice(c * NT, (c + 1) * NT)
            nc.vector.tensor_scalar(
                out=us[:, cols], in0=us[:, cols], scalar1=1.0 / 20.0, scalar2=None, op0=ALU.mult
            )
            nc.vector.tensor_scalar(
                out=mx[:, cols], in0=us[:, cols], scalar1=1.0 - K, scalar2=0.0, op0=ALU.mult, op1=ALU.min
            )

        def softmax_exp(c):
            for a in range(NT):
                i = c * NT + a
                nc.scalar.activation(
                    out=lgs[c][:, a, :], in_=kk[:], func=ACT.Exp, bias=mx[:, i : i + 1], scale=us[:, i : i + 1]
                )

        def softmax_sum(c):
            for a in range(NT):
                i = c * NT + a
                nc.vector.scalar_tensor_tensor(
                    out=lgs[c][:, a, :], in0=lgs[c][:, a, :], scalar=1.0, in1=lc[:], op0=ALU.mult, op1=ALU.mult,
                    accum_out=ssum[:, i : i + 1],
                )

        def softmax_end():
            nc.vector.reciprocal(out=rs[:], in_=ssum[:])
            nc.vector.tensor_scalar(out=rs[:], in0=rs[:], scalar1=-64.0, scalar2=None, op0=ALU.mult)

        xps = {}
        qs = {}
        ns = {}
        n2s = {}
        pulls = {}

        def at_x(i):
            ts = slice(i * P, (i + 1) * P)
            xps[i] = []
            for b in range(2):
                xp = psum.tile([P, 4, P], F32, name="bank")
                xps[i].append(xp)
                for rr in range(4):
                    terms = ((m2T, ident[:]), (nc2T, turned(4 * b + rr)))
                    for k, (src, moving) in enumerate(terms):
                        nc.tensor.matmul(
                            out=xp[:, rr, :], lhsT=src[:, ts], rhs=moving, is_transpose=True,
                            start=(k == 0), stop=(k == 1),
                        )

        def at_q(i):
            qs[i] = t4("q")
            for b in range(2):
                nc.scalar.activation(
                    out=qs[i][:, b * 512 : (b + 1) * 512], in_=xps[i][b][:].rearrange("p r k -> p (r k)"), func=ACT.Square
                )

        def gap_row(i, n):
            c, a = divmod(i, NT)
            return gaps[c][:, a].unsqueeze(1).to_broadcast([P, n, PAIRS * G])

        def by_gap(t):
            return t.rearrange("p (r j) -> p r j", j=PAIRS * G)

        def rk(t):
            return t.rearrange("p (r k) -> p r k", k=P)

        def at_n(i):
            ns[i] = t4("n")
            nc.vector.scalar_tensor_tensor(
                out=by_gap(ns[i][:]), in0=by_gap(qs[i][:]), scalar=2.0, in1=gap_row(i, KB4 // 64),
                op0=ALU.add, op1=ALU.subtract,
            )

        def at_n2(i):
            n2s[i] = t4("n2")
            nc.scalar.activation(out=n2s[i][:], in_=ns[i][:], func=ACT.Square)

        def at_xn(i):
            for b in range(2):
                half = slice(b * 512, (b + 1) * 512)
                nc.vector.tensor_mul(
                    out=qs[i][:, half], in0=xps[i][b][:].rearrange("p r k -> p (r k)"), in1=ns[i][:, half]
                )

        def at_d(i, part=slice(0, KB4)):
            cols = by_gap(n2s[i][:, part])
            nc.vector.scalar_tensor_tensor(
                out=cols, in0=gap_row(i, (part.stop - part.start) // 64), scalar=8.0, in1=cols,
                op0=ALU.mult, op1=ALU.add,
            )

        def at_rho(i, part=slice(0, KB4)):
            nc.scalar.activation(out=n2s[i][:, part], in_=n2s[i][:, part], func=ACT.Abs_reciprocal_sqrt)

        def at_r(i, part=slice(0, KB4)):
            nc.scalar.activation(out=n2s[i][:, part], in_=n2s[i][:, part], func=ACT.Square)

        def at_f(i, part=slice(0, PAIRS)):
            fb = fbufs[i % 3]
            spread = fb[:, 0 : PAIRS * (P + G)].rearrange("p (r x) -> p r x", x=P + G)[:, :, 0:P]
            nc.vector.tensor_mul(out=spread[:, part], in0=rk(qs[i][:])[:, part], in1=rk(n2s[i][:])[:, part])

        def at_sum(i):
            fb = fbufs[i % 3]
            pulls[i] = side.tile([P, P], F32, name="side")
            for r in range(PAIRS + 1):
                nc.tensor.matmul(
                    out=pulls[i][:], lhsT=fb[:, r * P : (r + 1) * P], rhs=ident[:], is_transpose=True,
                    start=(r == 0), stop=(r == PAIRS),
                )

        pls = {}
        c2s = {}
        outs = {}

        def end_copy(i):
            pls[i] = work.tile([P, P], F32, name="pl")
            nc.scalar.activation(out=pls[i][:], in_=pulls[i][:], func=ACT.Copy, scale=-0.5)

        def end_turn(i):
            c2s[i] = side.tile([P, P], F32, name="side")
            nc.tensor.matmul(out=c2s[i][:], lhsT=pls[i][:], rhs=backf, is_transpose=True, start=True, stop=False)
            nc.tensor.matmul(
                out=c2s[i][:], lhsT=nc2T[:, i * P : (i + 1) * P], rhs=ident[:], is_transpose=True, start=False, stop=True
            )

        def end_out(i):
            c, a = divmod(i, NT)
            if a == 0:
                outs[c] = work.tile([P, NT, K], F32, name="o")
            nc.vector.scalar_tensor_tensor(
                out=outs[c][:, a, :], in0=c2s[i][:], scalar=rs[:, i : i + 1], in1=lgs[c][:, a, :],
                op0=ALU.mult, op1=ALU.mult,
            )
            first_tile = {NT - 1: 0} if c < NCH - 1 else {NT - 2: 0, NT - 1: NT - 1}
            if a in first_tile:
                tiles = slice(first_tile[a], a + 1)
                nc.sync.dma_start(
                    out=out[c * CH : (c + 1) * CH, :].rearrange("(p a) k -> p a k", a=NT)[:, tiles, :],
                    in_=outs[c][:, tiles, :],
                )


        nc.gpsimd.memset(warm[:], 0.0)
        nc.scalar.activation(out=warm[:], in_=warm[:], func=ACT.Gelu)
        gpsimd_constants()
        nc.gpsimd.iota(kk[:], pattern=[[1, K]], base=0, channel_multiplier=0, allow_small_or_imprecise_dtypes=True)
        for fb in fbufs:
            rows = fb[:, 0 : PAIRS * (P + G)].rearrange("p (r x) -> p r x", x=P + G)
            nc.gpsimd.memset(rows[:, :, P : P + G], 0.0)
            nc.gpsimd.memset(fb[:, PAIRS * (P + G) : 9 * P], 0.0)

        def widen_pair(pr, on_scalar):
            for w in (2 * pr, 2 * pr + 1):
                widen(w // NT, w % NT, on_scalar)

        def turn_pair(pr):
            for w in (2 * pr, 2 * pr + 1):
                turn_x(w // NT, w % NT)

        widen(0, 0, 2)
        for w in range(1, NT):
            widen(0, w, 2)
            turn_x(0, w - 1)
        turn_x(0, NT - 1)
        for i in range(3):
            nc.vector.tensor_copy(out=vecf[:, i, :], in_=vecs[i][:].rearrange("p h t -> p (h t)"))
        permute(0, 0)
        permute_scales(0, nc.vector)
        permute(0, 1)
        for kg in range(2):
            quantize_x(0, kg)
        permute(0, 2)
        permute(0, 3)
        for j in range(2 * NCH):
            first(j // 2, j % 2)
            if j == 0:
                widen_pair(2, 2)
                turn_pair(2)
                for t in range(4):
                    permute(1, t)
                permute_scales(1, nc.vector)
                nc.vector.tensor_mul(out=gw[:], in0=vecf[:, 1, :], in1=vecf[:, 2, :])
                binomial_start()
            if j == 1:
                load_x(3)
            if j in (3, 5, 7):
                second((j - 3) // 2)
            if j >= 4:
                u_turn((j - 4) // 2, (j - 4) % 2)
            if j >= 1:
                gain((j - 1) // 2, (j - 1) % 2)
            if j in (1, 3, 5):
                quantize_x((j + 1) // 2, 0)
            if j + 3 < 2 * NCH:
                widen_pair(j + 3, (3, 3, 3, 3, 3)[j])
                turn_pair(j + 3)
            if j in (1, 3, 5):
                quantize_x((j + 1) // 2, 1)
            if j in (3, 5, 7):
                leave_second((j - 3) // 2)
            if j >= 6:
                weigh((j - 1) // 2, (j - 1) % 2)
            if j >= 1:
                quantize_h((j - 1) // 2, (j - 1) % 2)
            if j == 7:
                gain(3, 1)
            if 1 <= j < 6:
                weigh((j - 1) // 2, (j - 1) % 2)
            if j == 6:
                u_out(0)
                exponents(0)
        quantize_h(3, 1)
        second(3)
        u_turn(2, 0)
        u_turn(2, 1)
        weigh(3, 1)
        u_turn(3, 0)
        u_turn(3, 1)
        for c in range(3):
            softplus_exp(c)
        leave_second(3)
        softplus_exp(3)
        u_out(1)
        exponents(1)
        u_out(2)
        exponents(2)
        for c in range(NCH):
            softplus_ln(c)
        binomial_ln()
        softplus_a(0)
        pair_turn(0)
        softplus_c(0)
        pair_copy(0, False)
        mean_turn(0)
        pair_gap(0, False)
        binomial_end()
        u_out(3)
        exponents(3)
        mean_copy(0, False)
        at_x(0)
        softplus_a(1)
        pair_turn(1)
        softplus_c(1)
        for c in (2, 3):
            softplus_a(c)
            softplus_c(c)
        for c in range(NCH - 1):
            softmax_exp(c)
        at_q(0)
        softmax_exp(NCH - 1)
        binomial_exp()
        pair_copy(1, True)

        def attract_step(k):
            if k + 1 < TILES:
                at_q(k + 1)
            if 4 <= k:
                end_copy(k - 4)
            if k < TILES:
                at_n(k)
            if 5 <= k:
                end_out(k - 5)
            if k < TILES:
                at_xn(k)
            if k + 2 < TILES:
                at_x(k + 2)
            if 3 <= k < TILES + 3:
                at_f(k - 3)
            if 2 <= k < TILES + 2:
                at_rho(k - 2)
            if 1 <= k < TILES:
                at_d(k - 1)
            if k < TILES:
                at_n2(k)
            if 2 <= k < TILES + 2:
                at_r(k - 2)
            if 4 <= k:
                end_turn(k - 4)
            if 3 <= k < TILES + 3:
                at_sum(k - 3)

        at_x(1)
        for k in range(TILES):
            c, part = divmod(k + 6, 4)
            attract_step(k)
            if k < NCH:
                softmax_sum(k)
            if k == NCH - 1:
                softmax_end()
            if c < NCH:
                if part == 0:
                    pair_turn(c)
                elif part == 1:
                    pair_copy(c, True)
                elif part == 2:
                    mean_turn(c)
                    pair_gap(c, True)
                else:
                    mean_copy(c, True)

        last = TILES - 1
        halves = [slice(0, 512), slice(512, 1024)]
        at_rho(last - 1)
        for part in halves:
            at_d(last, part)
        end_copy(last - 3)
        at_f(last - 2)
        at_r(last - 1)
        end_turn(last - 3)
        at_sum(last - 2)
        end_out(last - 4)
        for part in halves:
            at_rho(last, part)
            at_r(last, part)
        at_f(last - 1)
        end_out(last - 3)
        end_copy(last - 2)
        end_turn(last - 2)
        at_sum(last - 1)
        for part in range(2):
            at_f(last, slice(4 * part, 4 * part + 4))
        at_sum(last)
        end_out(last - 2)
        for i in (last - 1, last):
            end_copy(i)
            end_turn(i)
            end_out(i)
